import numpy as np
import ml_dtypes


def mxq(x, axis, fmt="e4m3"):
    dtype, down = {"e4m3": (ml_dtypes.float8_e4m3fn, 7), "e5m2": (ml_dtypes.float8_e5m2, 14)}[fmt]
    v = np.moveaxis(np.asarray(x, np.float32).astype(ml_dtypes.bfloat16).astype(np.float64), axis, -1)
    blocks = v.reshape(v.shape[:-1] + (-1, 32))
    amax = np.abs(blocks).max(-1, keepdims=True)
    byte = np.maximum(np.where(amax > 0, np.frexp(amax)[1] - 1 + 127, 0) - down, 1)
    scale = np.exp2(byte - 127.0)
    codes = (blocks / scale).astype(np.float32).astype(dtype).astype(np.float64)
    return np.moveaxis((codes * scale).reshape(v.shape), -1, axis)


WIDE = False


def mx_kscale(k):
    if not WIDE:
        return np.ones(k)
    levels = np.array([10, -10, 5, -5, 0])
    if k % 512:
        return np.exp2(np.random.permutation(np.resize(levels, k // 32))).repeat(32)
    a = np.empty((k // 512, 16))
    for p in range(k // 512):
        a[p, :8] = np.random.permutation(np.resize(levels, 8))
        for g in range(8):
            far = levels[np.abs(levels - a[p, g]) >= 10]
            a[p, g + 8] = far[np.random.randint(len(far))]
    return np.exp2(a.ravel()).repeat(32)


BF16 = ml_dtypes.bfloat16


def bf(x):
    return np.asarray(x, np.float32).astype(BF16)


def f64(x):
    return np.asarray(x).astype(np.float64)


E2M1 = np.array([0.0, 0.5, 1.0, 1.5, 2.0, 3.0, 4.0, 6.0, -0.0, -0.5, -1.0, -1.5, -2.0, -3.0, -4.0, -6.0])


def pack_weight(w, fmt):
    k, n = w.shape
    w = f64(bf(w)).reshape(k // 32, 32, n)
    amax = np.abs(w).max(1)
    if fmt == "e4m3":
        byte = np.frexp(amax)[1] - 1 + 127 - 7
    else:
        mant, ex = np.frexp(amax / 6.0)
        byte = np.where(mant > 0.5, ex, ex - 1) + 127
    byte = np.clip(np.where(amax > 0, byte, 1), 1, 254)
    scaled = (w * np.exp2(127.0 - byte)[:, None, :]).reshape(k, n).astype(np.float32)
    by_word = np.ascontiguousarray(scaled.reshape(k // 512, 128, 4, n).transpose(0, 1, 3, 2))
    if fmt == "e4m3":
        words = by_word.astype(ml_dtypes.float8_e4m3fn).view(np.uint8)
    else:
        c = by_word.astype(ml_dtypes.float4_e2m1fn).view(np.uint8) & 0xF
        words = c[..., 0::2] | (c[..., 1::2] << 4)
    return np.ascontiguousarray(words), np.ascontiguousarray(byte.astype(np.uint8).reshape(k // 512, 16, n))


def unpack_weight(words, scales, fmt):
    g, p, n, _ = words.shape
    if fmt == "e4m3":
        vals = np.ascontiguousarray(words).view(ml_dtypes.float8_e4m3fn).astype(np.float64)
    else:
        nib = np.empty((g, p, n, 4), np.uint8)
        nib[..., 0::2] = words & 0xF
        nib[..., 1::2] = words >> 4
        vals = E2M1[nib]
    vals = vals * np.repeat(np.exp2(scales.astype(np.float64) - 127.0), 8, axis=1)[..., None]
    return vals.transpose(0, 1, 3, 2).reshape(g * 512, n)
def pack4(w):
    words, scales = pack_weight(w, "e2m1")
    return words.reshape(words.shape[0], 128, -1), scales


def unpack4(words, scales):
    return unpack_weight(words.reshape(words.shape[0], 128, -1, 2), scales, "e2m1")


E4M3FN = np.array([(-1.0 if i & 128 else 1.0) * ((1.0 + (i & 7) / 8.0) * 2.0 ** (((i >> 3) & 15) - 7) if i & 120 else (i & 7) * 2.0 ** -9) for i in range(256)])


def e4m3fn_bytes(y):
    return np.clip(np.asarray(y, np.float64), -448.0, 448.0).astype(np.float32).astype(ml_dtypes.float8_e4m3fn).view(np.uint8)


def e4m3fn_values(b):
    return E4M3FN[b]


T, N, D, F, R, K = 4, 512, 512, 512, 512, 3


def softmax(v):
    e = np.exp(v - v.max(-1, keepdims=True))
    return e / e.sum(-1, keepdims=True)


def transitions(edge, e1, e2):
    lg = np.maximum(e1 @ e2.T, 0.0)
    forward = softmax(edge)
    backward = softmax(edge.T)
    adaptive = softmax(lg)
    return np.stack([forward, backward, adaptive], axis=0)


def draw0():
    s, t, r = mx_kscale(D), mx_kscale(N), mx_kscale(R)
    c = np.sqrt(2.0) / R**0.25
    x = bf(np.random.standard_normal((T, N, D)) * s / t[:, None])
    edge = bf(np.random.standard_normal((N, N)) * 2.0)
    e1_words, e1_scales = pack4((np.random.standard_normal((N, R)) * c * r).T)
    e2_words, e2_scales = pack4((np.random.standard_normal((N, R)) * c / r).T)
    return {"x": x,
            "edge": edge,
            "e1_words": e1_words,
            "e1_scales": e1_scales,
            "e2_words": e2_words,
            "e2_scales": e2_scales,
            "w": bf(np.random.standard_normal((K, D, F)) / np.sqrt(D) / s[:, None]),
            "g": bf(np.random.standard_normal((K, N)) * 2.0 * t),
            "bias": bf(np.random.standard_normal(F) * 0.4)}


def core(x, edge, e1_words, e1_scales, e2_words, e2_scales, w, g, bias):
    e1 = unpack4(e1_words, e1_scales).T
    e2 = unpack4(e2_words, e2_scales).T
    p = transitions(f64(edge), e1, e2)
    q = p * f64(g)[:, None, :]
    h = mxq(f64(x), 2, "e4m3")[None] @ mxq(f64(w), 1, "e4m3")[:, None]
    z = mxq(q, 2, "e4m3")[:, None] @ mxq(h, 2, "e4m3")
    y = z[0] + z[1] + z[2] + f64(bias)
    return np.maximum(y, 0.0)


def setup_inputs():
    drawn = draw0()
    full = np.asarray(drawn['w']).astype(np.float64)
    scale = (np.abs(full).reshape(3, 4, 128, 4, 128).max(axis=(2, 4)) / 448.0).astype(np.float32)
    given = {}
    for key, value in drawn.items():
        if key == 'w':
            given['w_bytes'] = e4m3fn_bytes(full / np.repeat(np.repeat(scale.astype(np.float64), 128, axis=1), 128, axis=2))
            given['w_scale'] = scale
        else:
            given[key] = value
    return given


def reference(x, edge, e1_words, e1_scales, e2_words, e2_scales, w_bytes, w_scale, g, bias):
    return core(x, edge, e1_words, e1_scales, e2_words, e2_scales, e4m3fn_values(w_bytes) * np.repeat(np.repeat(w_scale.astype(np.float64), 128, axis=1), 128, axis=2), g, bias)

@@ -1,0 +1,306 @@
+from contextlib import ExitStack
+
+import concourse.mybir as mybir
+from concourse.masks import make_identity
+
+T, N, D, F, R, K = 4, 512, 512, 512, 512, 3
+FLOPS = 2 * N * N * R + K * T * (2 * N * D * F + 2 * N * N * F)
+
+F32 = mybir.dt.float32
+BF16 = mybir.dt.bfloat16
+U32 = mybir.dt.uint32
+I32 = mybir.dt.int32
+U8 = mybir.dt.uint8
+FP8 = mybir.dt.float8_e4m3fn
+FP8X4 = mybir.dt.float8_e4m3fn_x4
+FP4X4 = mybir.dt.float4_e2m1fn_x4
+ALU = mybir.AluOpType
+ACT = mybir.ActivationFunctionType
+X = mybir.AxisListType.X
+P = 128
+
+
+def tile_graphwavenetdiffusionconv_d2p_kernel(
+    tc, x, edge, e1_words, e1_scales, e2_words, e2_scales, w_bytes, w_scale, g, bias, out
+):
+    nc = tc.nc
+    with ExitStack() as ctx:
+        keep = ctx.enter_context(tc.tile_pool(name="keep", bufs=1))
+        stage = ctx.enter_context(tc.tile_pool(name="stage", bufs=2))
+        psum = ctx.enter_context(tc.psum_pool(name="psum", bufs=1))
+
+        x_sb = [keep.tile([P, 4, D], BF16, name=f"x_sb{t}", align_bytes=64) for t in range(T)]
+        w8 = [keep.tile([P, 4 * F], U8, name=f"w8_{k}", align_bytes=64) for k in range(K)]
+        ed = keep.tile([P, 4, N], BF16, name="ed", align_bytes=64)
+        gt = keep.tile([P, K, N], BF16, name="gt", align_bytes=64)
+        bt = keep.tile([P, F], BF16, name="bt", align_bytes=64)
+        ws = keep.tile([P, K, 4], F32, name="ws", align_bytes=64)
+        e1w = keep.tile([P, 2 * N], U8, name="e1w", align_bytes=64)
+        e2w = keep.tile([P, 2 * N], U8, name="e2w", align_bytes=64)
+        es = keep.tile([P, 2 * N], U8, name="es", align_bytes=64)
+
+        def load_x(t):
+            nc.sync.dma_start(out=x_sb[t][:], in_=x[t].rearrange("(m s) d -> m s d", s=4))
+
+        def load_w(k):
+            nc.sync.dma_start(out=w8[k][:].rearrange("p (j f) -> p j f", j=4), in_=w_bytes[k].rearrange("(p j) f -> p j f", j=4))
+
+        ident_f = keep.tile([P, P], F32, name="ident_f", align_bytes=64)
+        ident_b = keep.tile([P, P], BF16, name="ident_b", align_bytes=64)
+        make_identity(nc, ident_f[:])
+        make_identity(nc, ident_b[:])
+
+        load_w(0)
+        load_x(0)
+        nc.sync.dma_start(out=ed[:], in_=edge.rearrange("(a p) j -> p a j", p=P))
+        ws_rows = w_scale.rearrange("k i b -> i k b")
+        for q in range(4):
+            nc.gpsimd.dma_start(out=ws[32 * q : 32 * q + 32], in_=ws_rows[q].partition_broadcast(32))
+        nc.sync.dma_start(out=gt[:].rearrange("p k j -> p (k j)"), in_=g.rearrange("k j -> (k j)").partition_broadcast(P))
+        load_w(1)
+        load_w(2)
+        nc.gpsimd.memset(es[:].bitcast(I32), 0)
+        nc.sync.dma_start(out=e1w[:].bitcast(I32), in_=e1_words[0].bitcast(I32))
+        nc.sync.dma_start(out=e2w[:].bitcast(I32), in_=e2_words[0].bitcast(I32))
+        for q in range(4):
+            nc.sync.dma_start(out=es[32 * q : 32 * q + 4, 0:N].bitcast(I32), in_=e1_scales[0, 4 * q : 4 * q + 4, :].bitcast(I32))
+            nc.sync.dma_start(out=es[32 * q : 32 * q + 4, N : 2 * N].bitcast(I32), in_=e2_scales[0, 4 * q : 4 * q + 4, :].bitcast(I32))
+        load_x(1)
+        nc.sync.dma_start(out=bt[:], in_=bias.partition_broadcast(P))
+        load_x(2)
+        load_x(3)
+
+        def operand(name):
+            return (
+                keep.tile([P, 512], U32, name=name + "_c", align_bytes=64),
+                keep.tile([P, 512], U8, name=name + "_s", align_bytes=64),
+            )
+
+        xq = [operand(f"xq{t}") for t in range(T)]
+        wq = [operand(f"wq{k}") for k in range(K)]
+        qq = [operand(f"qq{k}") for k in range(K)]
+        hq = [[operand(f"hq{k}_{t}") for t in range(T)] for k in range(K)]
+
+        def quantize(op, grouped):
+            nc.vector.quantize_mx(
+                out=op[0][:].bitcast(FP8X4), scales=op[1][:], in_=grouped[:].rearrange("p c t -> p (c t)")
+            )
+
+        def copy(engine, out_, in_):
+            if engine == "v":
+                nc.vector.tensor_copy(out=out_, in_=in_)
+            else:
+                nc.scalar.copy(out=out_, in_=in_)
+
+        def turn(src, engines):
+            words = src[:].bitcast(F32)
+            grouped = stage.tile([P, 512, 4], BF16, name="turned", tag="turned", bufs=2, align_bytes=64)
+            gw = grouped[:].rearrange("p c t -> p (c t)").bitcast(F32)
+            for half in range(2):
+                bank = psum.tile([P, 2, 2, P], F32, name="bank", tag="m", bufs=4)
+                for s in range(2):
+                    for u in range(2):
+                        nc.tensor.transpose(bank[:, s, u, :], words[:, 2 * half + s, u::2], ident_f[:])
+                copy(
+                    engines[half],
+                    gw[:, 512 * half : 512 * half + 512].rearrange("p (s m u) -> p s m u", s=2, u=2),
+                    bank[:].rearrange("p s u m -> p s m u"),
+                )
+            return grouped
+
+        def prep_x(t, engines):
+            quantize(xq[t], turn(x_sb[t], engines))
+
+        def prep_w(k, cast):
+            wide = stage.tile([P, 4 * F], BF16, name="wide", tag="wide", bufs=2, align_bytes=64)
+            copy(cast, wide[:], w8[k][:].bitcast(FP8))
+            grouped = stage.tile([P, 512, 4], BF16, name="wgrp", tag="wgrp", bufs=2, align_bytes=64)
+            by_col = wide[:].rearrange("p (t f) -> p f t", t=4)
+            for b in range(4):
+                nc.vector.tensor_scalar(
+                    out=grouped[:, P * b : P * b + P, :],
+                    in0=by_col[:, P * b : P * b + P, :],
+                    scalar1=ws[:, k, b : b + 1],
+                    scalar2=None,
+                    op0=ALU.mult,
+                )
+            return grouped
+
+        E = [keep.tile([P, 4, N], F32, name=f"E{k}", align_bytes=64) for k in range(K)]
+        qb = [keep.tile([P, 4, N], BF16, name=f"qb{k}", align_bytes=64) for k in range(K)]
+        negmax = [keep.tile([P, 4], F32, name=f"negmax{k}", align_bytes=64) for k in range(K)]
+        total = [keep.tile([P, 4], F32, name=f"total{k}", align_bytes=64) for k in range(K)]
+        inv = [keep.tile([P, 4], F32, name=f"inv{k}", align_bytes=64) for k in range(K)]
+
+        def vmax(out_, a, b):
+            nc.vector.tensor_tensor(out=out_, in0=a, in1=b, op=ALU.max)
+
+        def row_max():
+            m1 = stage.tile([P, 4, 256], BF16, name="m1", tag="m1", bufs=1, align_bytes=64)
+            m2 = stage.tile([P, 4, 128], BF16, name="m2", tag="m2", bufs=1, align_bytes=64)
+            vmax(m1[:], ed[:, :, 0:256], ed[:, :, 256:512])
+            vmax(m2[:], m1[:, :, 0:128], m1[:, :, 128:256])
+            nc.vector.tensor_reduce(out=negmax[0][:], in_=m2[:], axis=X, op=ALU.max, negate=True)
+
+        def column_max():
+            c1 = stage.tile([P, 2, N], BF16, name="c1", tag="c1", bufs=1, align_bytes=64)
+            c2 = stage.tile([P, N], BF16, name="c2", tag="c2", bufs=1, align_bytes=64)
+            vmax(c1[:], ed[:, 0:2, :], ed[:, 2:4, :])
+            vmax(c2[:], c1[:, 0, :], c1[:, 1, :])
+            bank = psum.tile([P, 4, P], BF16, name="cmbank", tag="m", bufs=4)
+            for i in range(4):
+                nc.tensor.transpose(bank[:, i, :], c2[:, P * i : P * i + P], ident_b[:])
+            nc.vector.tensor_reduce(out=negmax[1][:], in_=bank[:], axis=X, op=ALU.max, negate=True)
+
+        def exps(k, i, src):
+            nc.scalar.activation(
+                out=E[k][:, i, :], in_=src, func=ACT.Exp, bias=negmax[k][:, i : i + 1], scale=1.0, accum_out=total[k][:, i : i + 1]
+            )
+
+        def exp0():
+            for i in range(4):
+                exps(0, i, ed[:, i, :])
+
+        def exp1():
+            for i in range(4):
+                bank = psum.tile([P, N], BF16, name="etbank", tag="m", bufs=4)
+                for a in range(4):
+                    nc.tensor.transpose(bank[:, P * a : P * a + P], ed[:, a, P * i : P * i + P], ident_b[:])
+                exps(1, i, bank[:])
+
+        rl = keep.tile([P, 4, N], F32, name="rl", align_bytes=64)
+        lgmax = keep.tile([P, 4], F32, name="lgmax", align_bytes=64)
+
+        def logits():
+            for i in range(4):
+                bank = psum.tile([P, N], F32, name="lgbank", tag="m", bufs=4)
+                nc.tensor.matmul_mx(
+                    out=bank[:],
+                    lhsT=e1w[:, 2 * P * i : 2 * P * i + 2 * P].bitcast(FP4X4),
+                    lhsT_scale=es[:, P * i : P * i + P],
+                    rhs=e2w[:].bitcast(FP4X4),
+                    rhs_scale=es[:, N : 2 * N],
+                    start=True,
+                    stop=True,
+                )
+                nc.vector.tensor_scalar(
+                    out=rl[:, i, :], in0=bank[:], scalar1=0.0, scalar2=None, op0=ALU.max, op1=ALU.max, accum_out=lgmax[:, i : i + 1]
+                )
+            nc.vector.tensor_scalar(out=negmax[2][:], in0=lgmax[:], scalar1=-1.0, scalar2=None, op0=ALU.mult)
+
+        def exp2():
+            for i in range(4):
+                exps(2, i, rl[:, i, :])
+
+        def finish_q(k, engines):
+            nc.vector.reciprocal(out=inv[k][:], in_=total[k][:])
+            for i in range(4):
+                nc.vector.scalar_tensor_tensor(
+                    out=qb[k][:, i, :], in0=E[k][:, i, :], scalar=inv[k][:, i : i + 1], in1=gt[:, k, :], op0=ALU.mult, op1=ALU.mult
+                )
+            quantize(qq[k], turn(qb[k], engines))
+
+        def h_step(k, t, engines):
+            grouped = stage.tile([P, 512, 4], BF16, name="hgrp", tag="hgrp", bufs=3, align_bytes=64)
+            for b in range(4):
+                bank = psum.tile([P, 4, P], F32, name="hbank", tag="h", bufs=4)
+                cols = slice(P * b, P * b + P)
+                for s in range(4):
+                    rows = slice(P * s, P * s + P)
+                    nc.tensor.matmul_mx(
+                        out=bank[:, s, :],
+                        lhsT=xq[t][0][:, rows].bitcast(FP8X4),
+                        lhsT_scale=xq[t][1][:, rows],
+                        rhs=wq[k][0][:, cols].bitcast(FP8X4),
+                        rhs_scale=wq[k][1][:, cols],
+                        start=True,
+                        stop=True,
+                    )
+                copy(engines[b], grouped[:, cols, :], bank[:].rearrange("p s f -> p f s"))
+            quantize(hq[k][t], grouped)
+
+        zb = [[None] * 4 for t in range(T)]
+
+        def z_step(k, t):
+            for i in range(4):
+                if k == 0:
+                    zb[t][i] = psum.tile([P, F], F32, name="zbank", tag="m", bufs=4)
+                rows = slice(P * i, P * i + P)
+                nc.tensor.matmul_mx(
+                    out=zb[t][i][:],
+                    lhsT=qq[k][0][:, rows].bitcast(FP8X4),
+                    lhsT_scale=qq[k][1][:, rows],
+                    rhs=hq[k][t][0][:].bitcast(FP8X4),
+                    rhs_scale=hq[k][t][1][:],
+                    start=(k == 0),
+                    stop=(k == K - 1),
+                )
+
+        def finish_z_by_tile(t):
+            for i in range(4):
+                ob = stage.tile([P, F], F32, name="ot", tag="ot", bufs=4, align_bytes=64)
+                nc.vector.tensor_tensor(out=ob[:], in0=zb[t][i][:], in1=bt[:], op=ALU.add)
+                if i % 2 == 0:
+                    nc.scalar.activation(out=ob[:], in_=ob[:], func=ACT.Relu)
+                else:
+                    nc.vector.tensor_scalar(out=ob[:], in0=ob[:], scalar1=0.0, scalar2=None, op0=ALU.max)
+                nc.sync.dma_start(out=out[t, P * i : P * i + P, :], in_=ob[:])
+
+        def finish_z(t):
+            for half in range(2):
+                ob = stage.tile([P, 2, F], F32, name="ob", tag="ob", bufs=3, align_bytes=64)
+                for i in range(2):
+                    nc.vector.tensor_tensor(out=ob[:, i, :], in0=zb[t][2 * half + i][:], in1=bt[:], op=ALU.add)
+                nc.vector.tensor_scalar(out=ob[:], in0=ob[:], scalar1=0.0, scalar2=None, op0=ALU.max)
+                nc.sync.dma_start(
+                    out=out[t, 2 * P * half : 2 * P * half + 2 * P, :].rearrange("(i p) f -> p i f", p=P), in_=ob[:]
+                )
+
+
+        g0 = prep_w(0, "v")
+        quantize(wq[0], g0)
+        prep_x(0, "ss")
+        row_max()
+        column_max()
+        h_step(0, 0, "ssss")
+        exp0()
+        g1 = prep_w(1, "s")
+        quantize(wq[1], g1)
+        exp1()
+        h_step(1, 0, "ssss")
+        logits()
+        finish_q(0, "ss")
+        g2 = prep_w(2, "s")
+        quantize(wq[2], g2)
+        exp2()
+        h_step(2, 0, "ssss")
+        finish_q(1, "ss")
+        prep_x(1, "ss")
+        h_step(0, 1, "ssss")
+        finish_q(2, "ss")
+        h_step(1, 1, "ssss")
+        z_step(0, 0)
+        z_step(1, 0)
+        z_step(2, 0)
+        h_step(2, 1, "ssss")
+        finish_z(0)
+        prep_x(2, "ss")
+        h_step(0, 2, "ssss")
+        z_step(0, 1)
+        z_step(1, 1)
+        z_step(2, 1)
+        finish_z(1)
+        h_step(1, 2, "ssss")
+        h_step(2, 2, "ssss")
+        prep_x(3, "ss")
+        z_step(0, 2)
+        z_step(1, 2)
+        h_step(0, 3, "ssss")
+        z_step(2, 2)
+        finish_z(2)
+        h_step(1, 3, "ssss")
+        z_step(0, 3)
+        h_step(2, 3, "svsv")
+        z_step(1, 3)
+        z_step(2, 3)
+        finish_z_by_tile(3)

@@ -28,7 +28,7 @@ def tile_graphwavenetdiffusionconv_d2p_kernel(
         keep = ctx.enter_context(tc.tile_pool(name="keep", bufs=1))
         stage = ctx.enter_context(tc.tile_pool(name="stage", bufs=2))
         psum = ctx.enter_context(tc.psum_pool(name="psum", bufs=1))
-
+        ctx.enter_context(tc.manual_schedule())
         x_sb = [keep.tile([P, 4, D], BF16, name=f"x_sb{t}", align_bytes=64) for t in range(T)]
         w8 = [keep.tile([P, 4 * F], U8, name=f"w8_{k}", align_bytes=64) for k in range(K)]
         ed = keep.tile([P, 4, N], BF16, name="ed", align_bytes=64)
@@ -38,6 +38,8 @@ def tile_graphwavenetdiffusionconv_d2p_kernel(
         e1w = keep.tile([P, 2 * N], U8, name="e1w", align_bytes=64)
         e2w = keep.tile([P, 2 * N], U8, name="e2w", align_bytes=64)
         es = keep.tile([P, 2 * N], U8, name="es", align_bytes=64)
+        ident_f = keep.tile([P, P], F32, name="ident_f", align_bytes=64)
+        ident_b = keep.tile([P, P], BF16, name="ident_b", align_bytes=64)
 
         def load_x(t):
             nc.sync.dma_start(out=x_sb[t][:], in_=x[t].rearrange("(m s) d -> m s d", s=4))
@@ -45,30 +47,27 @@ def tile_graphwavenetdiffusionconv_d2p_kernel(
         def load_w(k):
             nc.sync.dma_start(out=w8[k][:].rearrange("p (j f) -> p j f", j=4), in_=w_bytes[k].rearrange("(p j) f -> p j f", j=4))
 
-        ident_f = keep.tile([P, P], F32, name="ident_f", align_bytes=64)
-        ident_b = keep.tile([P, P], BF16, name="ident_b", align_bytes=64)
-        make_identity(nc, ident_f[:])
-        make_identity(nc, ident_b[:])
+        def load_edge():
+            nc.sync.dma_start(out=ed[:], in_=edge.rearrange("(a p) j -> p a j", p=P))
 
-        load_w(0)
-        load_x(0)
-        nc.sync.dma_start(out=ed[:], in_=edge.rearrange("(a p) j -> p a j", p=P))
-        ws_rows = w_scale.rearrange("k i b -> i k b")
-        for q in range(4):
-            nc.gpsimd.dma_start(out=ws[32 * q : 32 * q + 32], in_=ws_rows[q].partition_broadcast(32))
-        nc.sync.dma_start(out=gt[:].rearrange("p k j -> p (k j)"), in_=g.rearrange("k j -> (k j)").partition_broadcast(P))
-        load_w(1)
-        load_w(2)
-        nc.gpsimd.memset(es[:].bitcast(I32), 0)
-        nc.sync.dma_start(out=e1w[:].bitcast(I32), in_=e1_words[0].bitcast(I32))
-        nc.sync.dma_start(out=e2w[:].bitcast(I32), in_=e2_words[0].bitcast(I32))
-        for q in range(4):
-            nc.sync.dma_start(out=es[32 * q : 32 * q + 4, 0:N].bitcast(I32), in_=e1_scales[0, 4 * q : 4 * q + 4, :].bitcast(I32))
-            nc.sync.dma_start(out=es[32 * q : 32 * q + 4, N : 2 * N].bitcast(I32), in_=e2_scales[0, 4 * q : 4 * q + 4, :].bitcast(I32))
-        load_x(1)
-        nc.sync.dma_start(out=bt[:], in_=bias.partition_broadcast(P))
-        load_x(2)
-        load_x(3)
+        def load_ws(queue):
+            rows = w_scale.rearrange("k i b -> i k b")
+            for q in range(4):
+                queue.dma_start(out=ws[32 * q : 32 * q + 32], in_=rows[q].partition_broadcast(32))
+
+        def load_g():
+            nc.sync.dma_start(out=gt[:].rearrange("p k j -> p (k j)"), in_=g.rearrange("k j -> (k j)").partition_broadcast(P))
+
+        def load_bias():
+            nc.sync.dma_start(out=bt[:], in_=bias.partition_broadcast(P))
+
+        def load_e():
+            nc.sync.dma_start(out=e1w[:].bitcast(I32), in_=e1_words[0].bitcast(I32))
+            nc.sync.dma_start(out=e2w[:].bitcast(I32), in_=e2_words[0].bitcast(I32))
+            for q in range(4):
+                rows = slice(32 * q, 32 * q + 4)
+                nc.sync.dma_start(out=es[rows, 0:N].bitcast(I32), in_=e1_scales[0, 4 * q : 4 * q + 4, :].bitcast(I32))
+                nc.sync.dma_start(out=es[rows, N : 2 * N].bitcast(I32), in_=e2_scales[0, 4 * q : 4 * q + 4, :].bitcast(I32))
 
         def operand(name):
             return (
@@ -89,218 +88,426 @@ def tile_graphwavenetdiffusionconv_d2p_kernel(
         def copy(engine, out_, in_):
             if engine == "v":
                 nc.vector.tensor_copy(out=out_, in_=in_)
+            elif engine == "g":
+                nc.gpsimd.tensor_copy(out=out_, in_=in_)
             else:
                 nc.scalar.copy(out=out_, in_=in_)
 
-        def turn(src, engines):
+        def turn_half(src, grouped, half, engine):
             words = src[:].bitcast(F32)
-            grouped = stage.tile([P, 512, 4], BF16, name="turned", tag="turned", bufs=2, align_bytes=64)
             gw = grouped[:].rearrange("p c t -> p (c t)").bitcast(F32)
-            for half in range(2):
-                bank = psum.tile([P, 2, 2, P], F32, name="bank", tag="m", bufs=4)
-                for s in range(2):
-                    for u in range(2):
-                        nc.tensor.transpose(bank[:, s, u, :], words[:, 2 * half + s, u::2], ident_f[:])
-                copy(
-                    engines[half],
-                    gw[:, 512 * half : 512 * half + 512].rearrange("p (s m u) -> p s m u", s=2, u=2),
-                    bank[:].rearrange("p s u m -> p s m u"),
-                )
-            return grouped
+            bank = psum.tile([P, 2, 2, P], F32, name="bank", tag="m", bufs=4)
+            for s in range(2):
+                for u in range(2):
+                    nc.tensor.transpose(bank[:, s, u, :], words[:, 2 * half + s, u::2], ident_f[:])
+            copy(
+                engine,
+                gw[:, 512 * half : 512 * half + 512].rearrange("p (s m u) -> p s m u", s=2, u=2),
+                bank[:].rearrange("p s u m -> p s m u"),
+            )
 
-        def prep_x(t, engines):
-            quantize(xq[t], turn(x_sb[t], engines))
+        x_grp = {}
+        q_grp = {}
+        w_wide = {}
+        w_grp = {}
+        h_grp = {}
 
-        def prep_w(k, cast):
-            wide = stage.tile([P, 4 * F], BF16, name="wide", tag="wide", bufs=2, align_bytes=64)
-            copy(cast, wide[:], w8[k][:].bitcast(FP8))
-            grouped = stage.tile([P, 512, 4], BF16, name="wgrp", tag="wgrp", bufs=2, align_bytes=64)
-            by_col = wide[:].rearrange("p (t f) -> p f t", t=4)
+        def x_turn(t, half, engine="s"):
+            if t not in x_grp:
+                x_grp[t] = stage.tile([P, 512, 4], BF16, name="turned", tag="turned", bufs=5, align_bytes=64)
+            turn_half(x_sb[t], x_grp[t], half, engine)
+
+        def x_quant(t):
+            quantize(xq[t], x_grp[t])
+
+        def w_cast(k, engine):
+            w_wide[k] = stage.tile([P, 4 * F], BF16, name="wide", tag="wide", bufs=2, align_bytes=64)
+            copy(engine, w_wide[k][:], w8[k][:].bitcast(FP8))
+
+        def w_group(k):
+            w_grp[k] = stage.tile([P, 512, 4], BF16, name="wgrp", tag="wgrp", bufs=2, align_bytes=64)
+            by_col = w_wide[k][:].rearrange("p (t f) -> p f t", t=4)
             for b in range(4):
                 nc.vector.tensor_scalar(
-                    out=grouped[:, P * b : P * b + P, :],
+                    out=w_grp[k][:, P * b : P * b + P, :],
                     in0=by_col[:, P * b : P * b + P, :],
                     scalar1=ws[:, k, b : b + 1],
                     scalar2=None,
                     op0=ALU.mult,
                 )
-            return grouped
+
+        def w_quant(k):
+            quantize(wq[k], w_grp[k])
 
         E = [keep.tile([P, 4, N], F32, name=f"E{k}", align_bytes=64) for k in range(K)]
         qb = [keep.tile([P, 4, N], BF16, name=f"qb{k}", align_bytes=64) for k in range(K)]
         negmax = [keep.tile([P, 4], F32, name=f"negmax{k}", align_bytes=64) for k in range(K)]
         total = [keep.tile([P, 4], F32, name=f"total{k}", align_bytes=64) for k in range(K)]
         inv = [keep.tile([P, 4], F32, name=f"inv{k}", align_bytes=64) for k in range(K)]
+        rl = keep.tile([P, 4, N], F32, name="rl", align_bytes=64)
+        lgmax = keep.tile([P, 4], F32, name="lgmax", align_bytes=64)
+        m1 = keep.tile([P, 4, 256], BF16, name="m1", align_bytes=64)
+        m2 = keep.tile([P, 4, 128], BF16, name="m2", align_bytes=64)
+        c1 = keep.tile([P, 2, N], BF16, name="c1", align_bytes=64)
+        c2 = keep.tile([P, N], BF16, name="c2", align_bytes=64)
 
         def vmax(out_, a, b):
             nc.vector.tensor_tensor(out=out_, in0=a, in1=b, op=ALU.max)
 
-        def row_max():
-            m1 = stage.tile([P, 4, 256], BF16, name="m1", tag="m1", bufs=1, align_bytes=64)
-            m2 = stage.tile([P, 4, 128], BF16, name="m2", tag="m2", bufs=1, align_bytes=64)
-            vmax(m1[:], ed[:, :, 0:256], ed[:, :, 256:512])
-            vmax(m2[:], m1[:, :, 0:128], m1[:, :, 128:256])
-            nc.vector.tensor_reduce(out=negmax[0][:], in_=m2[:], axis=X, op=ALU.max, negate=True)
+        def max_step(n):
+            if n == 0:
+                vmax(m1[:], ed[:, :, 0:256], ed[:, :, 256:512])
+            if n == 1:
+                vmax(c1[:], ed[:, 0:2, :], ed[:, 2:4, :])
+            if n == 2:
+                vmax(m2[:], m1[:, :, 0:128], m1[:, :, 128:256])
+            if n == 3:
+                vmax(c2[:], c1[:, 0, :], c1[:, 1, :])
+            if n == 4:
+                nc.vector.tensor_reduce(out=negmax[0][:], in_=m2[:], axis=X, op=ALU.max, negate=True)
 
         def column_max():
-            c1 = stage.tile([P, 2, N], BF16, name="c1", tag="c1", bufs=1, align_bytes=64)
-            c2 = stage.tile([P, N], BF16, name="c2", tag="c2", bufs=1, align_bytes=64)
-            vmax(c1[:], ed[:, 0:2, :], ed[:, 2:4, :])
-            vmax(c2[:], c1[:, 0, :], c1[:, 1, :])
             bank = psum.tile([P, 4, P], BF16, name="cmbank", tag="m", bufs=4)
             for i in range(4):
                 nc.tensor.transpose(bank[:, i, :], c2[:, P * i : P * i + P], ident_b[:])
             nc.vector.tensor_reduce(out=negmax[1][:], in_=bank[:], axis=X, op=ALU.max, negate=True)
 
-        def exps(k, i, src):
+        def exps(k, i):
+            if k == 0:
+                src = ed[:, i, :]
+            elif k == 1:
+                bank = psum.tile([P, N], BF16, name="etbank", tag="m", bufs=4)
+                for a in range(4):
+                    nc.tensor.transpose(bank[:, P * a : P * a + P], ed[:, a, P * i : P * i + P], ident_b[:])
+                src = bank[:]
+            else:
+                src = rl[:, i, :]
             nc.scalar.activation(
                 out=E[k][:, i, :], in_=src, func=ACT.Exp, bias=negmax[k][:, i : i + 1], scale=1.0, accum_out=total[k][:, i : i + 1]
             )
 
-        def exp0():
-            for i in range(4):
-                exps(0, i, ed[:, i, :])
+        def logits(i):
+            bank = psum.tile([P, N], F32, name="lgbank", tag="m", bufs=4)
+            nc.tensor.matmul_mx(
+                out=bank[:],
+                lhsT=e1w[:, 2 * P * i : 2 * P * i + 2 * P].bitcast(FP4X4),
+                lhsT_scale=es[:, P * i : P * i + P],
+                rhs=e2w[:].bitcast(FP4X4),
+                rhs_scale=es[:, N : 2 * N],
+                start=True,
+                stop=True,
+            )
+            nc.vector.tensor_scalar(
+                out=rl[:, i, :], in0=bank[:], scalar1=0.0, scalar2=None, op0=ALU.max, op1=ALU.max, accum_out=lgmax[:, i : i + 1]
+            )
 
-        def exp1():
-            for i in range(4):
-                bank = psum.tile([P, N], BF16, name="etbank", tag="m", bufs=4)
-                for a in range(4):
-                    nc.tensor.transpose(bank[:, P * a : P * a + P], ed[:, a, P * i : P * i + P], ident_b[:])
-                exps(1, i, bank[:])
+        def logits_max():
+            nc.vector.tensor_scalar(out=negmax[2][:], in0=lgmax[:], scalar1=-1.0, scalar2=None, op0=ALU.mult)
 
-        rl = keep.tile([P, 4, N], F32, name="rl", align_bytes=64)
-        lgmax = keep.tile([P, 4], F32, name="lgmax", align_bytes=64)
+        def q_inv(k):
+            nc.vector.reciprocal(out=inv[k][:], in_=total[k][:])
 
-        def logits():
-            for i in range(4):
-                bank = psum.tile([P, N], F32, name="lgbank", tag="m", bufs=4)
+        def q_scale(k, i):
+            nc.vector.scalar_tensor_tensor(
+                out=qb[k][:, i, :], in0=E[k][:, i, :], scalar=inv[k][:, i : i + 1], in1=gt[:, k, :], op0=ALU.mult, op1=ALU.mult
+            )
+
+        def q_turn(k, half, engine="s"):
+            if k not in q_grp:
+                q_grp[k] = stage.tile([P, 512, 4], BF16, name="turned", tag="turned", bufs=5, align_bytes=64)
+            turn_half(qb[k], q_grp[k], half, engine)
+
+        def q_quant(k):
+            quantize(qq[k], q_grp[k])
+
+        def h_block(k, t, b, engine="s"):
+            if (k, t) not in h_grp:
+                h_grp[k, t] = stage.tile([P, 512, 4], BF16, name="hgrp", tag="hgrp", bufs=9, align_bytes=64)
+            bank = psum.tile([P, 4, P], F32, name="hbank", tag="h", bufs=4)
+            cols = slice(P * b, P * b + P)
+            for s in range(4):
+                rows = slice(P * s, P * s + P)
                 nc.tensor.matmul_mx(
-                    out=bank[:],
-                    lhsT=e1w[:, 2 * P * i : 2 * P * i + 2 * P].bitcast(FP4X4),
-                    lhsT_scale=es[:, P * i : P * i + P],
-                    rhs=e2w[:].bitcast(FP4X4),
-                    rhs_scale=es[:, N : 2 * N],
+                    out=bank[:, s, :],
+                    lhsT=xq[t][0][:, rows].bitcast(FP8X4),
+                    lhsT_scale=xq[t][1][:, rows],
+                    rhs=wq[k][0][:, cols].bitcast(FP8X4),
+                    rhs_scale=wq[k][1][:, cols],
                     start=True,
                     stop=True,
                 )
-                nc.vector.tensor_scalar(
-                    out=rl[:, i, :], in0=bank[:], scalar1=0.0, scalar2=None, op0=ALU.max, op1=ALU.max, accum_out=lgmax[:, i : i + 1]
-                )
-            nc.vector.tensor_scalar(out=negmax[2][:], in0=lgmax[:], scalar1=-1.0, scalar2=None, op0=ALU.mult)
+            copy(engine, h_grp[k, t][:, cols, :], bank[:].rearrange("p s f -> p f s"))
 
-        def exp2():
-            for i in range(4):
-                exps(2, i, rl[:, i, :])
-
-        def finish_q(k, engines):
-            nc.vector.reciprocal(out=inv[k][:], in_=total[k][:])
-            for i in range(4):
-                nc.vector.scalar_tensor_tensor(
-                    out=qb[k][:, i, :], in0=E[k][:, i, :], scalar=inv[k][:, i : i + 1], in1=gt[:, k, :], op0=ALU.mult, op1=ALU.mult
-                )
-            quantize(qq[k], turn(qb[k], engines))
-
-        def h_step(k, t, engines):
-            grouped = stage.tile([P, 512, 4], BF16, name="hgrp", tag="hgrp", bufs=3, align_bytes=64)
+        def h(k, t, engines="ssss"):
             for b in range(4):
-                bank = psum.tile([P, 4, P], F32, name="hbank", tag="h", bufs=4)
-                cols = slice(P * b, P * b + P)
-                for s in range(4):
-                    rows = slice(P * s, P * s + P)
-                    nc.tensor.matmul_mx(
-                        out=bank[:, s, :],
-                        lhsT=xq[t][0][:, rows].bitcast(FP8X4),
-                        lhsT_scale=xq[t][1][:, rows],
-                        rhs=wq[k][0][:, cols].bitcast(FP8X4),
-                        rhs_scale=wq[k][1][:, cols],
-                        start=True,
-                        stop=True,
-                    )
-                copy(engines[b], grouped[:, cols, :], bank[:].rearrange("p s f -> p f s"))
-            quantize(hq[k][t], grouped)
+                h_block(k, t, b, engines[b])
 
-        zb = [[None] * 4 for t in range(T)]
+        def h_quant(k, t):
+            quantize(hq[k][t], h_grp[k, t])
 
-        def z_step(k, t):
-            for i in range(4):
-                if k == 0:
-                    zb[t][i] = psum.tile([P, F], F32, name="zbank", tag="m", bufs=4)
-                rows = slice(P * i, P * i + P)
-                nc.tensor.matmul_mx(
-                    out=zb[t][i][:],
-                    lhsT=qq[k][0][:, rows].bitcast(FP8X4),
-                    lhsT_scale=qq[k][1][:, rows],
-                    rhs=hq[k][t][0][:].bitcast(FP8X4),
-                    rhs_scale=hq[k][t][1][:],
-                    start=(k == 0),
-                    stop=(k == K - 1),
-                )
+        z_bank = {}
+        z_done = {}
 
-        def finish_z_by_tile(t):
-            for i in range(4):
-                ob = stage.tile([P, F], F32, name="ot", tag="ot", bufs=4, align_bytes=64)
-                nc.vector.tensor_tensor(out=ob[:], in0=zb[t][i][:], in1=bt[:], op=ALU.add)
-                if i % 2 == 0:
-                    nc.scalar.activation(out=ob[:], in_=ob[:], func=ACT.Relu)
-                else:
-                    nc.vector.tensor_scalar(out=ob[:], in0=ob[:], scalar1=0.0, scalar2=None, op0=ALU.max)
-                nc.sync.dma_start(out=out[t, P * i : P * i + P, :], in_=ob[:])
+        def z_pass(k, t, i):
+            c = z_done.get((t, i), 0)
+            if c == 0:
+                z_bank[t, i] = psum.tile([P, F], F32, name="zbank", tag="m", bufs=4)
+            rows = slice(P * i, P * i + P)
+            nc.tensor.matmul_mx(
+                out=z_bank[t, i][:],
+                lhsT=qq[k][0][:, rows].bitcast(FP8X4),
+                lhsT_scale=qq[k][1][:, rows],
+                rhs=hq[k][t][0][:].bitcast(FP8X4),
+                rhs_scale=hq[k][t][1][:],
+                start=(c == 0),
+                stop=(c == K - 1),
+            )
+            z_done[t, i] = c + 1
 
-        def finish_z(t):
-            for half in range(2):
-                ob = stage.tile([P, 2, F], F32, name="ob", tag="ob", bufs=3, align_bytes=64)
-                for i in range(2):
-                    nc.vector.tensor_tensor(out=ob[:, i, :], in0=zb[t][2 * half + i][:], in1=bt[:], op=ALU.add)
-                nc.vector.tensor_scalar(out=ob[:], in0=ob[:], scalar1=0.0, scalar2=None, op0=ALU.max)
-                nc.sync.dma_start(
-                    out=out[t, 2 * P * half : 2 * P * half + 2 * P, :].rearrange("(i p) f -> p i f", p=P), in_=ob[:]
-                )
+        def z(t, i):
+            for k in range(K):
+                z_pass(k, t, i)
+
+        ob = {}
+
+        def z_add(t, i):
+            if (t, i // 2) not in ob:
+                ob[t, i // 2] = stage.tile([P, 2, F], F32, name="ob", tag="ob", bufs=6, align_bytes=64)
+            nc.vector.tensor_tensor(out=ob[t, i // 2][:, i % 2, :], in0=z_bank[t, i][:], in1=bt[:], op=ALU.add)
+
+        def relu(engine, ap):
+            if engine == "v":
+                nc.vector.tensor_scalar(out=ap, in0=ap, scalar1=0.0, scalar2=None, op0=ALU.max)
+            elif engine == "g":
+                nc.gpsimd.tensor_scalar(out=ap, in0=ap, scalar1=3.0e38, scalar2=0.0, op0=ALU.min, op1=ALU.max)
+            else:
+                nc.scalar.activation(out=ap, in_=ap, func=ACT.Relu)
+
+        def z_out(t, half, engine="v"):
+            relu(engine, ob[t, half][:])
+            nc.sync.dma_start(
+                out=out[t, 2 * P * half : 2 * P * half + 2 * P, :].rearrange("(i p) f -> p i f", p=P), in_=ob[t, half][:]
+            )
+
+        def z_out_tile(t, i, engine):
+            relu(engine, ob[t, i // 2][:, i % 2, :])
+            nc.sync.dma_start(out=out[t, P * i : P * i + P, :], in_=ob[t, i // 2][:, i % 2, :])
 
 
-        g0 = prep_w(0, "v")
-        quantize(wq[0], g0)
-        prep_x(0, "ss")
-        row_max()
+        make_identity(nc, ident_f[:])
+        make_identity(nc, ident_b[:])
+        load_w(0)
+        load_x(0)
+        load_edge()
+        load_ws(nc.gpsimd)
+        load_w(1)
+        load_x(1)
+        load_w(2)
+        load_x(2)
+        load_x(3)
+        nc.gpsimd.memset(es[:].bitcast(I32), 0)
+        load_e()
+        load_g()
+        load_bias()
+        x_turn(0, 0, "s")
+        x_turn(0, 1, "s")
+        w_cast(0, "v")
+        w_group(0)
+        max_step(0)
+        w_quant(0)
+        w_cast(1, "s")
+        max_step(1)
+        max_step(2)
+        max_step(3)
+        max_step(4)
+        w_cast(2, "s")
+        exps(0, 2)
+        exps(0, 1)
+        x_turn(1, 1, "v")
+        w_group(1)
         column_max()
-        h_step(0, 0, "ssss")
-        exp0()
-        g1 = prep_w(1, "s")
-        quantize(wq[1], g1)
-        exp1()
-        h_step(1, 0, "ssss")
-        logits()
-        finish_q(0, "ss")
-        g2 = prep_w(2, "s")
-        quantize(wq[2], g2)
-        exp2()
-        h_step(2, 0, "ssss")
-        finish_q(1, "ss")
-        prep_x(1, "ss")
-        h_step(0, 1, "ssss")
-        finish_q(2, "ss")
-        h_step(1, 1, "ssss")
-        z_step(0, 0)
-        z_step(1, 0)
-        z_step(2, 0)
-        h_step(2, 1, "ssss")
-        finish_z(0)
-        prep_x(2, "ss")
-        h_step(0, 2, "ssss")
-        z_step(0, 1)
-        z_step(1, 1)
-        z_step(2, 1)
-        finish_z(1)
-        h_step(1, 2, "ssss")
-        h_step(2, 2, "ssss")
-        prep_x(3, "ss")
-        z_step(0, 2)
-        z_step(1, 2)
-        h_step(0, 3, "ssss")
-        z_step(2, 2)
-        finish_z(2)
-        h_step(1, 3, "ssss")
-        z_step(0, 3)
-        h_step(2, 3, "svsv")
-        z_step(1, 3)
-        z_step(2, 3)
-        finish_z_by_tile(3)
+        exps(1, 0)
+        x_quant(0)
+        x_turn(1, 0, "s")
+        exps(1, 2)
+        x_turn(3, 1, "s")
+        w_group(2)
+        logits(1)
+        exps(0, 0)
+        logits(0)
+        exps(1, 3)
+        w_quant(2)
+        exps(0, 3)
+        h_block(0, 0, 3, "s")
+        x_quant(1)
+        w_quant(1)
+        q_inv(0)
+        logits(2)
+        exps(1, 1)
+        h_block(2, 0, 0, "s")
+        h_block(0, 1, 0, "s")
+        h_block(2, 1, 3, "v")
+        q_scale(0, 1)
+        logits(3)
+        logits_max()
+        h_block(0, 1, 1, "s")
+        x_turn(2, 0, "s")
+        q_scale(0, 0)
+        h_block(1, 1, 0, "s")
+        exps(2, 3)
+        h_block(1, 1, 2, "v")
+        h_block(2, 0, 3, "s")
+        q_inv(1)
+        h_block(1, 0, 2, "v")
+        x_turn(2, 1, "s")
+        h_block(1, 1, 3, "v")
+        exps(2, 0)
+        q_turn(0, 0, "v")
+        exps(2, 2)
+        h_block(2, 1, 2, "v")
+        x_quant(2)
+        exps(2, 1)
+        q_scale(1, 2)
+        h_block(0, 0, 0, "s")
+        x_turn(3, 0, "s")
+        h_block(0, 0, 2, "v")
+        h_block(2, 2, 0, "v")
+        h_block(0, 0, 1, "s")
+        q_scale(0, 3)
+        h_block(0, 1, 3, "s")
+        h_block(2, 2, 1, "s")
+        h_block(0, 2, 1, "s")
+        q_scale(1, 3)
+        q_inv(2)
+        q_scale(0, 2)
+        q_scale(1, 1)
+        h_block(2, 1, 0, "s")
+        x_quant(3)
+        h_block(2, 0, 1, "s")
+        q_scale(2, 1)
+        h_block(1, 0, 3, "s")
+        q_scale(2, 0)
+        h_block(1, 1, 1, "s")
+        q_scale(1, 0)
+        q_turn(1, 1, "s")
+        q_scale(2, 3)
+        q_scale(2, 2)
+        q_turn(0, 1, "s")
+        h_quant(0, 0)
+        h_block(2, 0, 2, "s")
+        h_block(1, 0, 0, "s")
+        q_quant(0)
+        h_block(0, 3, 2, "s")
+        h_block(1, 3, 1, "s")
+        q_turn(1, 0, "s")
+        q_turn(2, 0, "s")
+        q_turn(2, 1, "v")
+        h_block(1, 0, 1, "v")
+        h_quant(2, 0)
+        q_quant(2)
+        h_block(1, 3, 0, "s")
+        h_block(0, 2, 0, "s")
+        h_block(2, 3, 1, "v")
+        z_pass(0, 0, 0)
+        z_pass(0, 0, 2)
+        h_quant(1, 0)
+        q_quant(1)
+        h_block(0, 2, 2, "s")
+        z_pass(0, 0, 3)
+        h_block(0, 1, 2, "s")
+        z_pass(2, 0, 3)
+        h_block(2, 2, 3, "s")
+        h_block(1, 3, 2, "s")
+        z_pass(2, 0, 0)
+        h_block(2, 1, 1, "s")
+        z_pass(2, 0, 2)
+        h_quant(0, 1)
+        h_quant(1, 1)
+        h_block(2, 3, 3, "s")
+        z_pass(1, 0, 3)
+        z_add(0, 3)
+        h_block(1, 2, 3, "s")
+        z_pass(1, 0, 2)
+        h_block(1, 2, 2, "s")
+        z_pass(1, 1, 1)
+        z_pass(1, 0, 0)
+        z_add(0, 0)
+        h_block(2, 2, 2, "s")
+        h_block(2, 3, 0, "s")
+        h_quant(2, 1)
+        h_block(1, 3, 3, "s")
+        z_pass(0, 0, 1)
+        h_block(2, 3, 2, "s")
+        z_pass(0, 1, 1)
+        z_pass(2, 1, 1)
+        h_block(0, 3, 0, "s")
+        h_block(0, 3, 3, "s")
+        z_add(0, 2)
+        z_pass(2, 1, 3)
+        z_pass(2, 0, 1)
+        h_quant(2, 2)
+        z_add(1, 1)
+        h_block(1, 2, 1, "s")
+        z_pass(2, 1, 2)
+        h_quant(1, 3)
+        z_pass(1, 1, 0)
+        z_pass(0, 1, 0)
+        h_block(1, 2, 0, "s")
+        z_pass(1, 0, 1)
+        h_block(0, 2, 3, "s")
+        z_pass(1, 1, 2)
+        z_pass(0, 1, 3)
+        z_out(0, 1, "v")
+        h_quant(2, 3)
+        h_block(0, 3, 1, "s")
+        z_add(0, 1)
+        z_pass(2, 2, 3)
+        z_pass(1, 1, 3)
+        h_quant(1, 2)
+        z_pass(0, 1, 2)
+        h_quant(0, 2)
+        z_pass(1, 2, 3)
+        z_pass(2, 1, 0)
+        z_pass(0, 2, 3)
+        z_out(0, 0, "s")
+        z_add(1, 3)
+        z_pass(0, 2, 0)
+        z_pass(2, 2, 0)
+        z_pass(1, 2, 0)
+        z_add(1, 2)
+        z_add(1, 0)
+        z_out(1, 1, "s")
+        z_pass(1, 2, 1)
+        z_add(2, 3)
+        z_pass(2, 2, 1)
+        z_out(1, 0, "s")
+        z_pass(0, 2, 1)
+        z_pass(0, 2, 2)
+        z_add(2, 0)
+        z_add(2, 1)
+        z_pass(1, 2, 2)
+        z_pass(2, 2, 2)
+        z_pass(2, 3, 0)
+        z_pass(1, 3, 2)
+        z_pass(1, 3, 0)
+        z_pass(2, 3, 2)
+        h_quant(0, 3)
+        z_out(2, 0, "s")
+        z_pass(0, 3, 0)
+        z_add(2, 2)
+        z_out(2, 1, "v")
+        z_pass(2, 3, 1)
+        z_pass(0, 3, 2)
+        z_add(3, 0)
+        z_pass(1, 3, 1)
+        z_out_tile(3, 0, "s")
+        z_add(3, 2)
+        z_pass(0, 3, 1)
+        z_pass(0, 3, 3)
+        z_pass(1, 3, 3)
+        z_out_tile(3, 2, "s")
+        z_add(3, 1)
+        z_pass(2, 3, 3)
+        z_add(3, 3)
+        z_out_tile(3, 1, "s")
+        z_out_tile(3, 3, "s")

@@ -19,495 +19,393 @@ ACT = mybir.ActivationFunctionType
 X = mybir.AxisListType.X
 P = 128
 
-
 def tile_graphwavenetdiffusionconv_d2p_kernel(
     tc, x, edge, e1_words, e1_scales, e2_words, e2_scales, w_bytes, w_scale, g, bias, out
 ):
     nc = tc.nc
     with ExitStack() as ctx:
         keep = ctx.enter_context(tc.tile_pool(name="keep", bufs=1))
-        stage = ctx.enter_context(tc.tile_pool(name="stage", bufs=2))
+        stage = ctx.enter_context(tc.tile_pool(name="stage", bufs=1))
         psum = ctx.enter_context(tc.psum_pool(name="psum", bufs=1))
         ctx.enter_context(tc.manual_schedule())
-        x_sb = [keep.tile([P, 4, D], BF16, name=f"x_sb{t}", align_bytes=64) for t in range(T)]
-        w8 = [keep.tile([P, 4 * F], U8, name=f"w8_{k}", align_bytes=64) for k in range(K)]
-        ed = keep.tile([P, 4, N], BF16, name="ed", align_bytes=64)
-        gt = keep.tile([P, K, N], BF16, name="gt", align_bytes=64)
-        bt = keep.tile([P, F], BF16, name="bt", align_bytes=64)
-        ws = keep.tile([P, K, 4], F32, name="ws", align_bytes=64)
-        e1w = keep.tile([P, 2 * N], U8, name="e1w", align_bytes=64)
-        e2w = keep.tile([P, 2 * N], U8, name="e2w", align_bytes=64)
-        es = keep.tile([P, 2 * N], U8, name="es", align_bytes=64)
-        ident_f = keep.tile([P, P], F32, name="ident_f", align_bytes=64)
-        ident_b = keep.tile([P, P], BF16, name="ident_b", align_bytes=64)
 
-        def load_x(t):
-            nc.sync.dma_start(out=x_sb[t][:], in_=x[t].rearrange("(m s) d -> m s d", s=4))
-
-        def load_w(k):
-            nc.sync.dma_start(out=w8[k][:].rearrange("p (j f) -> p j f", j=4), in_=w_bytes[k].rearrange("(p j) f -> p j f", j=4))
-
-        def load_edge():
-            nc.sync.dma_start(out=ed[:], in_=edge.rearrange("(a p) j -> p a j", p=P))
-
-        def load_ws(queue):
-            rows = w_scale.rearrange("k i b -> i k b")
-            for q in range(4):
-                queue.dma_start(out=ws[32 * q : 32 * q + 32], in_=rows[q].partition_broadcast(32))
-
-        def load_g():
-            nc.sync.dma_start(out=gt[:].rearrange("p k j -> p (k j)"), in_=g.rearrange("k j -> (k j)").partition_broadcast(P))
-
-        def load_bias():
-            nc.sync.dma_start(out=bt[:], in_=bias.partition_broadcast(P))
-
-        def load_e():
-            nc.sync.dma_start(out=e1w[:].bitcast(I32), in_=e1_words[0].bitcast(I32))
-            nc.sync.dma_start(out=e2w[:].bitcast(I32), in_=e2_words[0].bitcast(I32))
-            for q in range(4):
-                rows = slice(32 * q, 32 * q + 4)
-                nc.sync.dma_start(out=es[rows, 0:N].bitcast(I32), in_=e1_scales[0, 4 * q : 4 * q + 4, :].bitcast(I32))
-                nc.sync.dma_start(out=es[rows, N : 2 * N].bitcast(I32), in_=e2_scales[0, 4 * q : 4 * q + 4, :].bitcast(I32))
+        def kept(name, shape, dtype):
+            return keep.tile([P] + shape, dtype, name=name, align_bytes=64)
 
         def operand(name):
-            return (
-                keep.tile([P, 512], U32, name=name + "_c", align_bytes=64),
-                keep.tile([P, 512], U8, name=name + "_s", align_bytes=64),
-            )
+            return kept(name + "_codes", [512], U32), kept(name + "_scales", [512], U8)
 
+        x_rows = [kept(f"x_rows{t}", [4, D], BF16) for t in range(T)]
+        w_raw = [kept(f"w_raw{k}", [4 * F], U8) for k in range(K)]
+        w_factor = kept("w_factor", [K, 4], F32)
+        edge_rows = kept("edge_rows", [4, N], BF16)
+        g_row = kept("g_row", [K, N], BF16)
+        ones = kept("ones", [P], BF16)
+        bias_all = kept("bias_all", [F], BF16)
+        e1_codes = kept("e1_codes", [2 * N], U8)
+        e2_codes = kept("e2_codes", [2 * N], U8)
+        e_scales = kept("e_scales", [2 * N], U8)
+        ident_f32 = kept("ident_f32", [P], F32)
+        ident_bf16 = kept("ident_bf16", [P], BF16)
+        half_max = kept("half_max", [4, 256], BF16)
+        quarter_max = kept("quarter_max", [4, 128], BF16)
+        pair_max = kept("pair_max", [2, N], BF16)
+        tile_max = kept("tile_max", [N], BF16)
+        lg_max = kept("lg_max", [4], F32)
+        neg_max = [kept(f"neg_max{k}", [4], F32) for k in range(K)]
+        exps = [kept(f"exps{k}", [4, N], F32) for k in range(K)]
+        exp_sum = [kept(f"exp_sum{k}", [4], F32) for k in range(K)]
+        inv_sum = [kept(f"inv_sum{k}", [4], F32) for k in range(K)]
+        q_rows = [kept(f"q_rows{k}", [4, N], BF16) for k in range(K)]
         xq = [operand(f"xq{t}") for t in range(T)]
         wq = [operand(f"wq{k}") for k in range(K)]
         qq = [operand(f"qq{k}") for k in range(K)]
         hq = [[operand(f"hq{k}_{t}") for t in range(T)] for k in range(K)]
+
+        x_grouped, w_wide, w_grouped, q_grouped, h_grouped, z_bank, relu_lg = {}, {}, {}, {}, {}, {}, {}
+
+        def load_x(t):
+            nc.sync.dma_start(out=x_rows[t][:], in_=x[t].rearrange("(m s) d -> m s d", s=4))
+
+        def load_w(k):
+            nc.sync.dma_start(
+                out=w_raw[k][:].rearrange("p (j f) -> p j f", j=4), in_=w_bytes[k].rearrange("(p j) f -> p j f", j=4)
+            )
+
+        def load_w_factor():
+            rows = w_scale.rearrange("k q b -> q k b")
+            for q in range(4):
+                nc.scalar.dma_start(out=w_factor[32 * q : 32 * q + 32], in_=rows[q].partition_broadcast(32))
+
+        def load_e():
+            nc.sync.dma_start(out=e1_codes[:].bitcast(I32), in_=e1_words[0].bitcast(I32))
+            nc.sync.dma_start(out=e2_codes[:].bitcast(I32), in_=e2_words[0].bitcast(I32))
+            for q in range(4):
+                for half, scales in enumerate((e1_scales, e2_scales)):
+                    nc.sync.dma_start(
+                        out=e_scales[32 * q : 32 * q + 4, N * half : N * half + N].bitcast(I32),
+                        in_=scales[0, 4 * q : 4 * q + 4, :].bitcast(I32),
+                    )
+
+        def copy(engine, out_, in_):
+            if engine == "v":
+                nc.vector.tensor_copy(out=out_, in_=in_)
+            else:
+                nc.scalar.copy(out=out_, in_=in_)
 
         def quantize(op, grouped):
             nc.vector.quantize_mx(
                 out=op[0][:].bitcast(FP8X4), scales=op[1][:], in_=grouped[:].rearrange("p c t -> p (c t)")
             )
 
-        def copy(engine, out_, in_):
-            if engine == "v":
-                nc.vector.tensor_copy(out=out_, in_=in_)
-            elif engine == "g":
-                nc.gpsimd.tensor_copy(out=out_, in_=in_)
-            else:
-                nc.scalar.copy(out=out_, in_=in_)
-
-        def turn_half(src, grouped, half, engine):
-            words = src[:].bitcast(F32)
-            gw = grouped[:].rearrange("p c t -> p (c t)").bitcast(F32)
-            bank = psum.tile([P, 2, 2, P], F32, name="bank", tag="m", bufs=4)
+        def turn_half(word_columns, rows, grouped, half, engine):
+            bank = psum.tile([P, 2, 2, P], F32, name="turn_bank", tag="work", bufs=4)
             for s in range(2):
                 for u in range(2):
-                    nc.tensor.transpose(bank[:, s, u, :], words[:, 2 * half + s, u::2], ident_f[:])
+                    nc.tensor.transpose(bank[:, s, u, :], word_columns(rows, 2 * half + s, u), ident_f32[:])
             copy(
                 engine,
-                gw[:, 512 * half : 512 * half + 512].rearrange("p (s m u) -> p s m u", s=2, u=2),
+                grouped[:].rearrange("p c t -> p (c t)").bitcast(F32)[:, 512 * half : 512 * half + 512].rearrange(
+                    "p (s m u) -> p s m u", s=2, u=2
+                ),
                 bank[:].rearrange("p s u m -> p s m u"),
             )
 
-        x_grp = {}
-        q_grp = {}
-        w_wide = {}
-        w_grp = {}
-        h_grp = {}
+        def turn(word_columns, rows, engines):
+            grouped = stage.tile([P, 512, 4], BF16, name="turned", tag="turned", bufs=5, align_bytes=64)
+            for half in range(2):
+                turn_half(word_columns, rows, grouped, half, engines[half])
+            return grouped
 
-        def x_turn(t, half, engine="s"):
-            if t not in x_grp:
-                x_grp[t] = stage.tile([P, 512, 4], BF16, name="turned", tag="turned", bufs=5, align_bytes=64)
-            turn_half(x_sb[t], x_grp[t], half, engine)
+        def turn_x(t, engines):
+            x_grouped[t] = turn(lambda rows, s, u: rows[:].bitcast(F32)[:, s, u::2], x_rows[t], engines)
 
-        def x_quant(t):
-            quantize(xq[t], x_grp[t])
+        def quantize_x(t):
+            quantize(xq[t], x_grouped[t])
 
-        def w_cast(k, engine):
-            w_wide[k] = stage.tile([P, 4 * F], BF16, name="wide", tag="wide", bufs=2, align_bytes=64)
-            copy(engine, w_wide[k][:], w8[k][:].bitcast(FP8))
+        def widen_w(k, engine):
+            w_wide[k] = stage.tile([P, 4 * F], BF16, name="wide", tag="wide", bufs=3, align_bytes=64)
+            copy(engine, w_wide[k][:], w_raw[k][:].bitcast(FP8))
 
-        def w_group(k):
-            w_grp[k] = stage.tile([P, 512, 4], BF16, name="wgrp", tag="wgrp", bufs=2, align_bytes=64)
-            by_col = w_wide[k][:].rearrange("p (t f) -> p f t", t=4)
+        def scale_w(k):
+            w_grouped[k] = stage.tile([P, 512, 4], BF16, name="wgrp", tag="wgrp", bufs=2, align_bytes=64)
+            by_column = w_wide[k][:].rearrange("p (t f) -> p f t", t=4)
             for b in range(4):
+                cols = slice(P * b, P * b + P)
                 nc.vector.tensor_scalar(
-                    out=w_grp[k][:, P * b : P * b + P, :],
-                    in0=by_col[:, P * b : P * b + P, :],
-                    scalar1=ws[:, k, b : b + 1],
+                    out=w_grouped[k][:, cols, :],
+                    in0=by_column[:, cols, :],
+                    scalar1=w_factor[:, k, b : b + 1],
                     scalar2=None,
                     op0=ALU.mult,
                 )
 
-        def w_quant(k):
-            quantize(wq[k], w_grp[k])
+        def quantize_w(k):
+            quantize(wq[k], w_grouped[k])
 
-        E = [keep.tile([P, 4, N], F32, name=f"E{k}", align_bytes=64) for k in range(K)]
-        qb = [keep.tile([P, 4, N], BF16, name=f"qb{k}", align_bytes=64) for k in range(K)]
-        negmax = [keep.tile([P, 4], F32, name=f"negmax{k}", align_bytes=64) for k in range(K)]
-        total = [keep.tile([P, 4], F32, name=f"total{k}", align_bytes=64) for k in range(K)]
-        inv = [keep.tile([P, 4], F32, name=f"inv{k}", align_bytes=64) for k in range(K)]
-        rl = keep.tile([P, 4, N], F32, name="rl", align_bytes=64)
-        lgmax = keep.tile([P, 4], F32, name="lgmax", align_bytes=64)
-        m1 = keep.tile([P, 4, 256], BF16, name="m1", align_bytes=64)
-        m2 = keep.tile([P, 4, 128], BF16, name="m2", align_bytes=64)
-        c1 = keep.tile([P, 2, N], BF16, name="c1", align_bytes=64)
-        c2 = keep.tile([P, N], BF16, name="c2", align_bytes=64)
+        def vector_max(out_, in0, in1):
+            nc.vector.tensor_tensor(out=out_, in0=in0, in1=in1, op=ALU.max)
 
-        def vmax(out_, a, b):
-            nc.vector.tensor_tensor(out=out_, in0=a, in1=b, op=ALU.max)
+        def row_max():
+            vector_max(half_max[:], edge_rows[:, :, 0:256], edge_rows[:, :, 256:512])
+            vector_max(quarter_max[:], half_max[:, :, 0:128], half_max[:, :, 128:256])
+            nc.vector.tensor_reduce(out=neg_max[0][:], in_=quarter_max[:], axis=X, op=ALU.max, negate=True)
 
-        def max_step(n):
-            if n == 0:
-                vmax(m1[:], ed[:, :, 0:256], ed[:, :, 256:512])
-            if n == 1:
-                vmax(c1[:], ed[:, 0:2, :], ed[:, 2:4, :])
-            if n == 2:
-                vmax(m2[:], m1[:, :, 0:128], m1[:, :, 128:256])
-            if n == 3:
-                vmax(c2[:], c1[:, 0, :], c1[:, 1, :])
-            if n == 4:
-                nc.vector.tensor_reduce(out=negmax[0][:], in_=m2[:], axis=X, op=ALU.max, negate=True)
+        def column_max_in_partitions():
+            vector_max(pair_max[:], edge_rows[:, 0:2, :], edge_rows[:, 2:4, :])
+            vector_max(tile_max[:], pair_max[:, 0, :], pair_max[:, 1, :])
 
         def column_max():
-            bank = psum.tile([P, 4, P], BF16, name="cmbank", tag="m", bufs=4)
+            bank = psum.tile([P, 4, P], BF16, name="max_bank", tag="work", bufs=4)
             for i in range(4):
-                nc.tensor.transpose(bank[:, i, :], c2[:, P * i : P * i + P], ident_b[:])
-            nc.vector.tensor_reduce(out=negmax[1][:], in_=bank[:], axis=X, op=ALU.max, negate=True)
+                nc.tensor.transpose(bank[:, i, :], tile_max[:, P * i : P * i + P], ident_bf16[:])
+            nc.vector.tensor_reduce(out=neg_max[1][:], in_=bank[:], axis=X, op=ALU.max, negate=True)
 
-        def exps(k, i):
-            if k == 0:
-                src = ed[:, i, :]
-            elif k == 1:
-                bank = psum.tile([P, N], BF16, name="etbank", tag="m", bufs=4)
-                for a in range(4):
-                    nc.tensor.transpose(bank[:, P * a : P * a + P], ed[:, a, P * i : P * i + P], ident_b[:])
-                src = bank[:]
-            else:
-                src = rl[:, i, :]
-            nc.scalar.activation(
-                out=E[k][:, i, :], in_=src, func=ACT.Exp, bias=negmax[k][:, i : i + 1], scale=1.0, accum_out=total[k][:, i : i + 1]
-            )
-
-        def logits(i):
-            bank = psum.tile([P, N], F32, name="lgbank", tag="m", bufs=4)
-            nc.tensor.matmul_mx(
-                out=bank[:],
-                lhsT=e1w[:, 2 * P * i : 2 * P * i + 2 * P].bitcast(FP4X4),
-                lhsT_scale=es[:, P * i : P * i + P],
-                rhs=e2w[:].bitcast(FP4X4),
-                rhs_scale=es[:, N : 2 * N],
-                start=True,
-                stop=True,
-            )
-            nc.vector.tensor_scalar(
-                out=rl[:, i, :], in0=bank[:], scalar1=0.0, scalar2=None, op0=ALU.max, op1=ALU.max, accum_out=lgmax[:, i : i + 1]
-            )
-
-        def logits_max():
-            nc.vector.tensor_scalar(out=negmax[2][:], in0=lgmax[:], scalar1=-1.0, scalar2=None, op0=ALU.mult)
-
-        def q_inv(k):
-            nc.vector.reciprocal(out=inv[k][:], in_=total[k][:])
-
-        def q_scale(k, i):
-            nc.vector.scalar_tensor_tensor(
-                out=qb[k][:, i, :], in0=E[k][:, i, :], scalar=inv[k][:, i : i + 1], in1=gt[:, k, :], op0=ALU.mult, op1=ALU.mult
-            )
-
-        def q_turn(k, half, engine="s"):
-            if k not in q_grp:
-                q_grp[k] = stage.tile([P, 512, 4], BF16, name="turned", tag="turned", bufs=5, align_bytes=64)
-            turn_half(qb[k], q_grp[k], half, engine)
-
-        def q_quant(k):
-            quantize(qq[k], q_grp[k])
-
-        def h_block(k, t, b, engine="s"):
-            if (k, t) not in h_grp:
-                h_grp[k, t] = stage.tile([P, 512, 4], BF16, name="hgrp", tag="hgrp", bufs=9, align_bytes=64)
-            bank = psum.tile([P, 4, P], F32, name="hbank", tag="h", bufs=4)
-            cols = slice(P * b, P * b + P)
-            for s in range(4):
-                rows = slice(P * s, P * s + P)
+        def logits(half):
+            relu_lg[half] = stage.tile([P, 2, N], F32, name="relu_lg", tag="out_rows", bufs=6, align_bytes=64)
+            for i in (2 * half, 2 * half + 1):
+                bank = psum.tile([P, N], F32, name="lg_bank", tag="work", bufs=4)
                 nc.tensor.matmul_mx(
-                    out=bank[:, s, :],
-                    lhsT=xq[t][0][:, rows].bitcast(FP8X4),
-                    lhsT_scale=xq[t][1][:, rows],
-                    rhs=wq[k][0][:, cols].bitcast(FP8X4),
-                    rhs_scale=wq[k][1][:, cols],
+                    out=bank[:],
+                    lhsT=e1_codes[:, 2 * P * i : 2 * P * i + 2 * P].bitcast(FP4X4),
+                    lhsT_scale=e_scales[:, P * i : P * i + P],
+                    rhs=e2_codes[:].bitcast(FP4X4),
+                    rhs_scale=e_scales[:, N : 2 * N],
                     start=True,
                     stop=True,
                 )
-            copy(engine, h_grp[k, t][:, cols, :], bank[:].rearrange("p s f -> p f s"))
+                nc.vector.tensor_scalar(
+                    out=relu_lg[half][:, i % 2, :],
+                    in0=bank[:],
+                    scalar1=0.0,
+                    scalar2=None,
+                    op0=ALU.max,
+                    op1=ALU.max,
+                    accum_out=lg_max[:, i : i + 1],
+                )
+            if half == 1:
+                nc.vector.tensor_scalar(out=neg_max[2][:], in0=lg_max[:], scalar1=-1.0, scalar2=None, op0=ALU.mult)
 
-        def h(k, t, engines="ssss"):
-            for b in range(4):
-                h_block(k, t, b, engines[b])
+        def word_order(row):
+            return row.rearrange("p (w u e) -> p u w e", u=2, e=2)
 
-        def h_quant(k, t):
-            quantize(hq[k][t], h_grp[k, t])
+        def exponentials(k, half):
+            for i in (2 * half, 2 * half + 1):
+                if k == 0:
+                    row = edge_rows[:, i, :]
+                elif k == 1:
+                    bank = psum.tile([P, N], BF16, name="edge_bank", tag="work", bufs=4)
+                    for a in range(4):
+                        nc.tensor.transpose(
+                            bank[:, P * a : P * a + P], edge_rows[:, a, P * i : P * i + P], ident_bf16[:]
+                        )
+                    row = bank[:]
+                else:
+                    row = relu_lg[half][:, i % 2, :]
+                nc.scalar.activation(
+                    out=exps[k][:, i, :].rearrange("p (u w e) -> p u w e", u=2, e=2),
+                    in_=word_order(row),
+                    func=ACT.Exp,
+                    bias=neg_max[k][:, i : i + 1],
+                    scale=1.0,
+                    accum_out=exp_sum[k][:, i : i + 1],
+                )
 
-        z_bank = {}
-        z_done = {}
-
-        def z_pass(k, t, i):
-            c = z_done.get((t, i), 0)
-            if c == 0:
-                z_bank[t, i] = psum.tile([P, F], F32, name="zbank", tag="m", bufs=4)
-            rows = slice(P * i, P * i + P)
-            nc.tensor.matmul_mx(
-                out=z_bank[t, i][:],
-                lhsT=qq[k][0][:, rows].bitcast(FP8X4),
-                lhsT_scale=qq[k][1][:, rows],
-                rhs=hq[k][t][0][:].bitcast(FP8X4),
-                rhs_scale=hq[k][t][1][:],
-                start=(c == 0),
-                stop=(c == K - 1),
+        def scale_q(k, half):
+            if half == 0:
+                nc.vector.reciprocal(out=inv_sum[k][:], in_=exp_sum[k][:])
+            bank = psum.tile([P, N], F32, name="g_bank", tag="work", bufs=4)
+            nc.tensor.matmul(
+                bank[:].rearrange("p (u w e) -> p u w e", u=2, e=2),
+                lhsT=ones[:],
+                rhs=word_order(g_row[:, k, :]),
+                start=True,
+                stop=True,
             )
-            z_done[t, i] = c + 1
+            for i in (2 * half, 2 * half + 1):
+                nc.vector.scalar_tensor_tensor(
+                    out=q_rows[k][:, i, :],
+                    in0=exps[k][:, i, :],
+                    scalar=inv_sum[k][:, i : i + 1],
+                    in1=bank[:],
+                    op0=ALU.mult,
+                    op1=ALU.mult,
+                )
 
-        def z(t, i):
-            for k in range(K):
-                z_pass(k, t, i)
+        def turn_q(k, engines):
+            q_grouped[k] = turn(lambda rows, s, u: rows[:].bitcast(F32)[:, s, P * u : P * u + P], q_rows[k], engines)
 
-        ob = {}
+        def quantize_q(k):
+            quantize(qq[k], q_grouped[k])
 
-        def z_add(t, i):
-            if (t, i // 2) not in ob:
-                ob[t, i // 2] = stage.tile([P, 2, F], F32, name="ob", tag="ob", bufs=6, align_bytes=64)
-            nc.vector.tensor_tensor(out=ob[t, i // 2][:, i % 2, :], in0=z_bank[t, i][:], in1=bt[:], op=ALU.add)
+        def multiply_h(k, t, half, engines):
+            if (k, t) not in h_grouped:
+                h_grouped[k, t] = stage.tile([P, 512, 4], BF16, name="hgrp", tag="hgrp", bufs=9, align_bytes=64)
+            for b, engine in zip((2 * half, 2 * half + 1), engines):
+                bank = psum.tile([P, 4, P], F32, name="h_bank", tag="h", bufs=4)
+                cols = slice(P * b, P * b + P)
+                for s in range(4):
+                    nodes = slice(P * s, P * s + P)
+                    nc.tensor.matmul_mx(
+                        out=bank[:, s, :],
+                        lhsT=xq[t][0][:, nodes].bitcast(FP8X4),
+                        lhsT_scale=xq[t][1][:, nodes],
+                        rhs=wq[k][0][:, cols].bitcast(FP8X4),
+                        rhs_scale=wq[k][1][:, cols],
+                        start=True,
+                        stop=True,
+                    )
+                copy(engine, h_grouped[k, t][:, cols, :], bank[:].rearrange("p s f -> p f s"))
+
+        def quantize_h(k, t):
+            quantize(hq[k][t], h_grouped[k, t])
+
+        def multiply_z(k, t, first=False, last=False):
+            for i in range(4):
+                if first:
+                    z_bank[t, i] = psum.tile([P, F], F32, name="z_bank", tag="work", bufs=4)
+                rows = slice(P * i, P * i + P)
+                nc.tensor.matmul_mx(
+                    out=z_bank[t, i][:],
+                    lhsT=qq[k][0][:, rows].bitcast(FP8X4),
+                    lhsT_scale=qq[k][1][:, rows],
+                    rhs=hq[k][t][0][:].bitcast(FP8X4),
+                    rhs_scale=hq[k][t][1][:],
+                    start=first,
+                    stop=last,
+                )
 
         def relu(engine, ap):
             if engine == "v":
                 nc.vector.tensor_scalar(out=ap, in0=ap, scalar1=0.0, scalar2=None, op0=ALU.max)
-            elif engine == "g":
-                nc.gpsimd.tensor_scalar(out=ap, in0=ap, scalar1=3.0e38, scalar2=0.0, op0=ALU.min, op1=ALU.max)
             else:
                 nc.scalar.activation(out=ap, in_=ap, func=ACT.Relu)
 
-        def z_out(t, half, engine="v"):
-            relu(engine, ob[t, half][:])
-            nc.sync.dma_start(
-                out=out[t, 2 * P * half : 2 * P * half + 2 * P, :].rearrange("(i p) f -> p i f", p=P), in_=ob[t, half][:]
-            )
+        def finish(t, half, engines):
+            rows = stage.tile([P, 2, F], F32, name="out_rows", tag="out_rows", bufs=6, align_bytes=64)
+            for i in range(2):
+                nc.vector.tensor_tensor(out=rows[:, i, :], in0=z_bank[t, 2 * half + i][:], in1=bias_all[:], op=ALU.add)
+            if len(engines) == 2:
+                for i in range(2):
+                    relu(engines[i], rows[:, i, :])
+                    first_row = P * (2 * half + i)
+                    nc.sync.dma_start(out=out[t, first_row : first_row + P, :], in_=rows[:, i, :])
+            else:
+                relu(engines, rows[:])
+                nc.sync.dma_start(
+                    out=out[t, 2 * P * half : 2 * P * half + 2 * P, :].rearrange("(i p) f -> p i f", p=P), in_=rows[:]
+                )
 
-        def z_out_tile(t, i, engine):
-            relu(engine, ob[t, i // 2][:, i % 2, :])
-            nc.sync.dma_start(out=out[t, P * i : P * i + P, :], in_=ob[t, i // 2][:, i % 2, :])
-
-
-        make_identity(nc, ident_f[:])
-        make_identity(nc, ident_b[:])
+        nc.gpsimd.memset(g_row[:], 0.0)
+        nc.gpsimd.memset(e_scales[:].bitcast(I32), 0)
+        make_identity(nc, ident_f32[:])
+        make_identity(nc, ident_bf16[:])
+        nc.gpsimd.memset(ones[:], 1.0)
+        load_w(2)
+        load_w_factor()
+        load_w(1)
+        nc.sync.dma_start(out=edge_rows[:], in_=edge.rearrange("(a p) j -> p a j", p=P))
         load_w(0)
         load_x(0)
-        load_edge()
-        load_ws(nc.gpsimd)
-        load_w(1)
-        load_x(1)
-        load_w(2)
         load_x(2)
+        nc.sync.dma_start(out=g_row[0:1], in_=g.rearrange("(o k) j -> o k j", o=1))
+        load_x(1)
         load_x(3)
-        nc.gpsimd.memset(es[:].bitcast(I32), 0)
         load_e()
-        load_g()
-        load_bias()
-        x_turn(0, 0, "s")
-        x_turn(0, 1, "s")
-        w_cast(0, "v")
-        w_group(0)
-        max_step(0)
-        w_quant(0)
-        w_cast(1, "s")
-        max_step(1)
-        max_step(2)
-        max_step(3)
-        max_step(4)
-        w_cast(2, "s")
-        exps(0, 2)
-        exps(0, 1)
-        x_turn(1, 1, "v")
-        w_group(1)
+        nc.sync.dma_start(out=bias_all[:], in_=bias.partition_broadcast(P))
+        widen_w(1, "v")
+        widen_w(2, "s")
+        row_max()
+        scale_w(1)
+        widen_w(0, "s")
+        scale_w(2)
+        exponentials(0, 1)
+        turn_x(0, "ss")
+        turn_x(2, "ss")
+        quantize_w(1)
+        turn_x(1, "ss")
+        turn_x(3, "ss")
+        quantize_w(2)
+        quantize_x(0)
+        column_max_in_partitions()
+        quantize_x(1)
+        multiply_h(1, 0, 1, "sv")
+        scale_w(0)
         column_max()
-        exps(1, 0)
-        x_quant(0)
-        x_turn(1, 0, "s")
-        exps(1, 2)
-        x_turn(3, 1, "s")
-        w_group(2)
-        logits(1)
-        exps(0, 0)
         logits(0)
-        exps(1, 3)
-        w_quant(2)
-        exps(0, 3)
-        h_block(0, 0, 3, "s")
-        x_quant(1)
-        w_quant(1)
-        q_inv(0)
-        logits(2)
-        exps(1, 1)
-        h_block(2, 0, 0, "s")
-        h_block(0, 1, 0, "s")
-        h_block(2, 1, 3, "v")
-        q_scale(0, 1)
-        logits(3)
-        logits_max()
-        h_block(0, 1, 1, "s")
-        x_turn(2, 0, "s")
-        q_scale(0, 0)
-        h_block(1, 1, 0, "s")
-        exps(2, 3)
-        h_block(1, 1, 2, "v")
-        h_block(2, 0, 3, "s")
-        q_inv(1)
-        h_block(1, 0, 2, "v")
-        x_turn(2, 1, "s")
-        h_block(1, 1, 3, "v")
-        exps(2, 0)
-        q_turn(0, 0, "v")
-        exps(2, 2)
-        h_block(2, 1, 2, "v")
-        x_quant(2)
-        exps(2, 1)
-        q_scale(1, 2)
-        h_block(0, 0, 0, "s")
-        x_turn(3, 0, "s")
-        h_block(0, 0, 2, "v")
-        h_block(2, 2, 0, "v")
-        h_block(0, 0, 1, "s")
-        q_scale(0, 3)
-        h_block(0, 1, 3, "s")
-        h_block(2, 2, 1, "s")
-        h_block(0, 2, 1, "s")
-        q_scale(1, 3)
-        q_inv(2)
-        q_scale(0, 2)
-        q_scale(1, 1)
-        h_block(2, 1, 0, "s")
-        x_quant(3)
-        h_block(2, 0, 1, "s")
-        q_scale(2, 1)
-        h_block(1, 0, 3, "s")
-        q_scale(2, 0)
-        h_block(1, 1, 1, "s")
-        q_scale(1, 0)
-        q_turn(1, 1, "s")
-        q_scale(2, 3)
-        q_scale(2, 2)
-        q_turn(0, 1, "s")
-        h_quant(0, 0)
-        h_block(2, 0, 2, "s")
-        h_block(1, 0, 0, "s")
-        q_quant(0)
-        h_block(0, 3, 2, "s")
-        h_block(1, 3, 1, "s")
-        q_turn(1, 0, "s")
-        q_turn(2, 0, "s")
-        q_turn(2, 1, "v")
-        h_block(1, 0, 1, "v")
-        h_quant(2, 0)
-        q_quant(2)
-        h_block(1, 3, 0, "s")
-        h_block(0, 2, 0, "s")
-        h_block(2, 3, 1, "v")
-        z_pass(0, 0, 0)
-        z_pass(0, 0, 2)
-        h_quant(1, 0)
-        q_quant(1)
-        h_block(0, 2, 2, "s")
-        z_pass(0, 0, 3)
-        h_block(0, 1, 2, "s")
-        z_pass(2, 0, 3)
-        h_block(2, 2, 3, "s")
-        h_block(1, 3, 2, "s")
-        z_pass(2, 0, 0)
-        h_block(2, 1, 1, "s")
-        z_pass(2, 0, 2)
-        h_quant(0, 1)
-        h_quant(1, 1)
-        h_block(2, 3, 3, "s")
-        z_pass(1, 0, 3)
-        z_add(0, 3)
-        h_block(1, 2, 3, "s")
-        z_pass(1, 0, 2)
-        h_block(1, 2, 2, "s")
-        z_pass(1, 1, 1)
-        z_pass(1, 0, 0)
-        z_add(0, 0)
-        h_block(2, 2, 2, "s")
-        h_block(2, 3, 0, "s")
-        h_quant(2, 1)
-        h_block(1, 3, 3, "s")
-        z_pass(0, 0, 1)
-        h_block(2, 3, 2, "s")
-        z_pass(0, 1, 1)
-        z_pass(2, 1, 1)
-        h_block(0, 3, 0, "s")
-        h_block(0, 3, 3, "s")
-        z_add(0, 2)
-        z_pass(2, 1, 3)
-        z_pass(2, 0, 1)
-        h_quant(2, 2)
-        z_add(1, 1)
-        h_block(1, 2, 1, "s")
-        z_pass(2, 1, 2)
-        h_quant(1, 3)
-        z_pass(1, 1, 0)
-        z_pass(0, 1, 0)
-        h_block(1, 2, 0, "s")
-        z_pass(1, 0, 1)
-        h_block(0, 2, 3, "s")
-        z_pass(1, 1, 2)
-        z_pass(0, 1, 3)
-        z_out(0, 1, "v")
-        h_quant(2, 3)
-        h_block(0, 3, 1, "s")
-        z_add(0, 1)
-        z_pass(2, 2, 3)
-        z_pass(1, 1, 3)
-        h_quant(1, 2)
-        z_pass(0, 1, 2)
-        h_quant(0, 2)
-        z_pass(1, 2, 3)
-        z_pass(2, 1, 0)
-        z_pass(0, 2, 3)
-        z_out(0, 0, "s")
-        z_add(1, 3)
-        z_pass(0, 2, 0)
-        z_pass(2, 2, 0)
-        z_pass(1, 2, 0)
-        z_add(1, 2)
-        z_add(1, 0)
-        z_out(1, 1, "s")
-        z_pass(1, 2, 1)
-        z_add(2, 3)
-        z_pass(2, 2, 1)
-        z_out(1, 0, "s")
-        z_pass(0, 2, 1)
-        z_pass(0, 2, 2)
-        z_add(2, 0)
-        z_add(2, 1)
-        z_pass(1, 2, 2)
-        z_pass(2, 2, 2)
-        z_pass(2, 3, 0)
-        z_pass(1, 3, 2)
-        z_pass(1, 3, 0)
-        z_pass(2, 3, 2)
-        h_quant(0, 3)
-        z_out(2, 0, "s")
-        z_pass(0, 3, 0)
-        z_add(2, 2)
-        z_out(2, 1, "v")
-        z_pass(2, 3, 1)
-        z_pass(0, 3, 2)
-        z_add(3, 0)
-        z_pass(1, 3, 1)
-        z_out_tile(3, 0, "s")
-        z_add(3, 2)
-        z_pass(0, 3, 1)
-        z_pass(0, 3, 3)
-        z_pass(1, 3, 3)
-        z_out_tile(3, 2, "s")
-        z_add(3, 1)
-        z_pass(2, 3, 3)
-        z_add(3, 3)
-        z_out_tile(3, 1, "s")
-        z_out_tile(3, 3, "s")
+        exponentials(0, 0)
+        multiply_h(2, 0, 1, "ss")
+        multiply_h(1, 0, 0, "sv")
+        quantize_x(2)
+        quantize_w(0)
+        multiply_h(2, 1, 1, "ss")
+        exponentials(1, 0)
+        logits(1)
+        multiply_h(2, 1, 0, "ss")
+        multiply_h(0, 0, 1, "sv")
+        multiply_h(0, 1, 1, "ss")
+        exponentials(2, 1)
+        scale_q(0, 0)
+        multiply_h(0, 2, 1, "vs")
+        multiply_h(2, 2, 1, "sv")
+        scale_q(0, 1)
+        exponentials(1, 1)
+        multiply_h(1, 2, 0, "ss")
+        multiply_h(1, 2, 1, "vv")
+        scale_q(1, 0)
+        turn_q(0, "ss")
+        exponentials(2, 0)
+        multiply_h(1, 1, 1, "vs")
+        multiply_h(0, 0, 0, "vs")
+        scale_q(1, 1)
+        scale_q(2, 0)
+        scale_q(2, 1)
+        multiply_h(2, 0, 0, "ss")
+        quantize_x(3)
+        quantize_h(0, 0)
+        multiply_h(0, 1, 0, "ss")
+        quantize_q(0)
+        multiply_h(0, 2, 0, "ss")
+        turn_q(1, "ss")
+        quantize_h(1, 0)
+        quantize_q(1)
+        turn_q(2, "ss")
+        multiply_h(1, 1, 0, "ss")
+        quantize_h(2, 0)
+        multiply_h(0, 3, 1, "vs")
+        multiply_z(0, 0, first=True)
+        quantize_q(2)
+        multiply_z(1, 0)
+        multiply_h(2, 2, 0, "ss")
+        multiply_z(2, 0, last=True)
+        multiply_h(0, 3, 0, "ss")
+        quantize_h(0, 1)
+        quantize_h(1, 1)
+        multiply_h(1, 3, 0, "ss")
+        finish(0, 0, "s")
+        finish(0, 1, "v")
+        multiply_z(1, 1, first=True)
+        multiply_z(0, 1)
+        quantize_h(2, 1)
+        quantize_h(1, 2)
+        quantize_h(2, 2)
+        multiply_z(2, 1, last=True)
+        finish(1, 0, "s")
+        multiply_h(1, 3, 1, "ss")
+        multiply_h(2, 3, 0, "ss")
+        finish(1, 1, "s")
+        multiply_z(1, 2, first=True)
+        quantize_h(0, 2)
+        multiply_z(2, 2)
+        multiply_z(0, 2, last=True)
+        quantize_h(0, 3)
+        multiply_h(2, 3, 1, "ss")
+        quantize_h(1, 3)
+        finish(2, 0, "s")
+        finish(2, 1, "s")
+        quantize_h(2, 3)
+        multiply_z(0, 3, first=True)
+        multiply_z(1, 3)
+        multiply_z(2, 3, last=True)
+        finish(3, 0, "ss")
+        finish(3, 1, "sv")

from contextlib import ExitStack

import concourse.mybir as mybir
from concourse.masks import make_identity

T, N, D, F, R, K = 4, 512, 512, 512, 512, 3
FLOPS = 2 * N * N * R + K * T * (2 * N * D * F + 2 * N * N * F)

F32 = mybir.dt.float32
BF16 = mybir.dt.bfloat16
U32 = mybir.dt.uint32
I32 = mybir.dt.int32
U8 = mybir.dt.uint8
FP8 = mybir.dt.float8_e4m3fn
FP8X4 = mybir.dt.float8_e4m3fn_x4
FP4X4 = mybir.dt.float4_e2m1fn_x4
ALU = mybir.AluOpType
ACT = mybir.ActivationFunctionType
X = mybir.AxisListType.X
P = 128

def tile_graphwavenetdiffusionconv_d2p_kernel(
    tc, x, edge, e1_words, e1_scales, e2_words, e2_scales, w_bytes, w_scale, g, bias, out
):
    nc = tc.nc
    with ExitStack() as ctx:
        keep = ctx.enter_context(tc.tile_pool(name="keep", bufs=1))
        stage = ctx.enter_context(tc.tile_pool(name="stage", bufs=1))
        psum = ctx.enter_context(tc.psum_pool(name="psum", bufs=1))
        ctx.enter_context(tc.manual_schedule())

        def kept(name, shape, dtype):
            return keep.tile([P] + shape, dtype, name=name, align_bytes=64)

        def operand(name):
            return kept(name + "_codes", [512], U32), kept(name + "_scales", [512], U8)

        x_rows = [kept(f"x_rows{t}", [4, D], BF16) for t in range(T)]
        w_raw = [kept(f"w_raw{k}", [4 * F], U8) for k in range(K)]
        w_factor = kept("w_factor", [K, 4], F32)
        edge_rows = kept("edge_rows", [4, N], BF16)
        g_row = kept("g_row", [K, N], BF16)
        ones = kept("ones", [P], BF16)
        bias_all = kept("bias_all", [F], BF16)
        e1_codes = kept("e1_codes", [2 * N], U8)
        e2_codes = kept("e2_codes", [2 * N], U8)
        e_scales = kept("e_scales", [2 * N], U8)
        ident_f32 = kept("ident_f32", [P], F32)
        ident_bf16 = kept("ident_bf16", [P], BF16)
        half_max = kept("half_max", [4, 256], BF16)
        quarter_max = kept("quarter_max", [4, 128], BF16)
        pair_max = kept("pair_max", [2, N], BF16)
        tile_max = kept("tile_max", [N], BF16)
        lg_max = kept("lg_max", [4], F32)
        neg_max = [kept(f"neg_max{k}", [4], F32) for k in range(K)]
        exps = [kept(f"exps{k}", [4, N], F32) for k in range(K)]
        exp_sum = [kept(f"exp_sum{k}", [4], F32) for k in range(K)]
        inv_sum = [kept(f"inv_sum{k}", [4], F32) for k in range(K)]
        q_rows = [kept(f"q_rows{k}", [4, N], BF16) for k in range(K)]
        xq = [operand(f"xq{t}") for t in range(T)]
        wq = [operand(f"wq{k}") for k in range(K)]
        qq = [operand(f"qq{k}") for k in range(K)]
        hq = [[operand(f"hq{k}_{t}") for t in range(T)] for k in range(K)]

        x_grouped, w_wide, w_grouped, q_grouped, h_grouped, z_bank, relu_lg = {}, {}, {}, {}, {}, {}, {}

        def load_x(t):
            nc.sync.dma_start(out=x_rows[t][:], in_=x[t].rearrange("(m s) d -> m s d", s=4))

        def load_w(k):
            nc.sync.dma_start(
                out=w_raw[k][:].rearrange("p (j f) -> p j f", j=4), in_=w_bytes[k].rearrange("(p j) f -> p j f", j=4)
            )

        def load_w_factor():
            rows = w_scale.rearrange("k q b -> q k b")
            for q in range(4):
                nc.scalar.dma_start(out=w_factor[32 * q : 32 * q + 32], in_=rows[q].partition_broadcast(32))

        def load_e():
            nc.sync.dma_start(out=e1_codes[:].bitcast(I32), in_=e1_words[0].bitcast(I32))
            nc.sync.dma_start(out=e2_codes[:].bitcast(I32), in_=e2_words[0].bitcast(I32))
            for q in range(4):
                for half, scales in enumerate((e1_scales, e2_scales)):
                    nc.sync.dma_start(
                        out=e_scales[32 * q : 32 * q + 4, N * half : N * half + N].bitcast(I32),
                        in_=scales[0, 4 * q : 4 * q + 4, :].bitcast(I32),
                    )

        def copy(engine, out_, in_):
            if engine == "v":
                nc.vector.tensor_copy(out=out_, in_=in_)
            else:
                nc.scalar.copy(out=out_, in_=in_)

        def quantize(op, grouped):
            nc.vector.quantize_mx(
                out=op[0][:].bitcast(FP8X4), scales=op[1][:], in_=grouped[:].rearrange("p c t -> p (c t)")
            )

        def turn_half(word_columns, rows, grouped, half, engine):
            bank = psum.tile([P, 2, 2, P], F32, name="turn_bank", tag="work", bufs=4)
            for s in range(2):
                for u in range(2):
                    nc.tensor.transpose(bank[:, s, u, :], word_columns(rows, 2 * half + s, u), ident_f32[:])
            copy(
                engine,
                grouped[:].rearrange("p c t -> p (c t)").bitcast(F32)[:, 512 * half : 512 * half + 512].rearrange(
                    "p (s m u) -> p s m u", s=2, u=2
                ),
                bank[:].rearrange("p s u m -> p s m u"),
            )

        def turn(word_columns, rows, engines):
            grouped = stage.tile([P, 512, 4], BF16, name="turned", tag="turned", bufs=5, align_bytes=64)
            for half in range(2):
                turn_half(word_columns, rows, grouped, half, engines[half])
            return grouped

        def turn_x(t, engines):
            x_grouped[t] = turn(lambda rows, s, u: rows[:].bitcast(F32)[:, s, u::2], x_rows[t], engines)

        def quantize_x(t):
            quantize(xq[t], x_grouped[t])

        def widen_w(k, engine):
            w_wide[k] = stage.tile([P, 4 * F], BF16, name="wide", tag="wide", bufs=3, align_bytes=64)
            copy(engine, w_wide[k][:], w_raw[k][:].bitcast(FP8))

        def scale_w(k):
            w_grouped[k] = stage.tile([P, 512, 4], BF16, name="wgrp", tag="wgrp", bufs=2, align_bytes=64)
            by_column = w_wide[k][:].rearrange("p (t f) -> p f t", t=4)
            for b in range(4):
                cols = slice(P * b, P * b + P)
                nc.vector.tensor_scalar(
                    out=w_grouped[k][:, cols, :],
                    in0=by_column[:, cols, :],
                    scalar1=w_factor[:, k, b : b + 1],
                    scalar2=None,
                    op0=ALU.mult,
                )

        def quantize_w(k):
            quantize(wq[k], w_grouped[k])

        def vector_max(out_, in0, in1):
            nc.vector.tensor_tensor(out=out_, in0=in0, in1=in1, op=ALU.max)

        def row_max():
            vector_max(half_max[:], edge_rows[:, :, 0:256], edge_rows[:, :, 256:512])
            vector_max(quarter_max[:], half_max[:, :, 0:128], half_max[:, :, 128:256])
            nc.vector.tensor_reduce(out=neg_max[0][:], in_=quarter_max[:], axis=X, op=ALU.max, negate=True)

        def column_max_in_partitions():
            vector_max(pair_max[:], edge_rows[:, 0:2, :], edge_rows[:, 2:4, :])
            vector_max(tile_max[:], pair_max[:, 0, :], pair_max[:, 1, :])

        def column_max():
            bank = psum.tile([P, 4, P], BF16, name="max_bank", tag="work", bufs=4)
            for i in range(4):
                nc.tensor.transpose(bank[:, i, :], tile_max[:, P * i : P * i + P], ident_bf16[:])
            nc.vector.tensor_reduce(out=neg_max[1][:], in_=bank[:], axis=X, op=ALU.max, negate=True)

        def logits(half):
            relu_lg[half] = stage.tile([P, 2, N], F32, name="relu_lg", tag="out_rows", bufs=6, align_bytes=64)
            for i in (2 * half, 2 * half + 1):
                bank = psum.tile([P, N], F32, name="lg_bank", tag="work", bufs=4)
                nc.tensor.matmul_mx(
                    out=bank[:],
                    lhsT=e1_codes[:, 2 * P * i : 2 * P * i + 2 * P].bitcast(FP4X4),
                    lhsT_scale=e_scales[:, P * i : P * i + P],
                    rhs=e2_codes[:].bitcast(FP4X4),
                    rhs_scale=e_scales[:, N : 2 * N],
                    start=True,
                    stop=True,
                )
                nc.vector.tensor_scalar(
                    out=relu_lg[half][:, i % 2, :],
                    in0=bank[:],
                    scalar1=0.0,
                    scalar2=None,
                    op0=ALU.max,
                    op1=ALU.max,
                    accum_out=lg_max[:, i : i + 1],
                )
            if half == 1:
                nc.vector.tensor_scalar(out=neg_max[2][:], in0=lg_max[:], scalar1=-1.0, scalar2=None, op0=ALU.mult)

        def word_order(row):
            return row.rearrange("p (w u e) -> p u w e", u=2, e=2)

        def exponentials(k, half):
            for i in (2 * half, 2 * half + 1):
                if k == 0:
                    row = edge_rows[:, i, :]
                elif k == 1:
                    bank = psum.tile([P, N], BF16, name="edge_bank", tag="work", bufs=4)
                    for a in range(4):
                        nc.tensor.transpose(
                            bank[:, P * a : P * a + P], edge_rows[:, a, P * i : P * i + P], ident_bf16[:]
                        )
                    row = bank[:]
                else:
                    row = relu_lg[half][:, i % 2, :]
                nc.scalar.activation(
                    out=exps[k][:, i, :].rearrange("p (u w e) -> p u w e", u=2, e=2),
                    in_=word_order(row),
                    func=ACT.Exp,
                    bias=neg_max[k][:, i : i + 1],
                    scale=1.0,
                    accum_out=exp_sum[k][:, i : i + 1],
                )

        def scale_q(k, half):
            if half == 0:
                nc.vector.reciprocal(out=inv_sum[k][:], in_=exp_sum[k][:])
            bank = psum.tile([P, N], F32, name="g_bank", tag="work", bufs=4)
            nc.tensor.matmul(
                bank[:].rearrange("p (u w e) -> p u w e", u=2, e=2),
                lhsT=ones[:],
                rhs=word_order(g_row[:, k, :]),
                start=True,
                stop=True,
            )
            for i in (2 * half, 2 * half + 1):
                nc.vector.scalar_tensor_tensor(
                    out=q_rows[k][:, i, :],
                    in0=exps[k][:, i, :],
                    scalar=inv_sum[k][:, i : i + 1],
                    in1=bank[:],
                    op0=ALU.mult,
                    op1=ALU.mult,
                )

        def turn_q(k, engines):
            q_grouped[k] = turn(lambda rows, s, u: rows[:].bitcast(F32)[:, s, P * u : P * u + P], q_rows[k], engines)

        def quantize_q(k):
            quantize(qq[k], q_grouped[k])

        def multiply_h(k, t, half, engines):
            if (k, t) not in h_grouped:
                h_grouped[k, t] = stage.tile([P, 512, 4], BF16, name="hgrp", tag="hgrp", bufs=9, align_bytes=64)
            for b, engine in zip((2 * half, 2 * half + 1), engines):
                bank = psum.tile([P, 4, P], F32, name="h_bank", tag="h", bufs=4)
                cols = slice(P * b, P * b + P)
                for s in range(4):
                    nodes = slice(P * s, P * s + P)
                    nc.tensor.matmul_mx(
                        out=bank[:, s, :],
                        lhsT=xq[t][0][:, nodes].bitcast(FP8X4),
                        lhsT_scale=xq[t][1][:, nodes],
                        rhs=wq[k][0][:, cols].bitcast(FP8X4),
                        rhs_scale=wq[k][1][:, cols],
                        start=True,
                        stop=True,
                    )
                copy(engine, h_grouped[k, t][:, cols, :], bank[:].rearrange("p s f -> p f s"))

        def quantize_h(k, t):
            quantize(hq[k][t], h_grouped[k, t])

        def multiply_z(k, t, first=False, last=False):
            for i in range(4):
                if first:
                    z_bank[t, i] = psum.tile([P, F], F32, name="z_bank", tag="work", bufs=4)
                rows = slice(P * i, P * i + P)
                nc.tensor.matmul_mx(
                    out=z_bank[t, i][:],
                    lhsT=qq[k][0][:, rows].bitcast(FP8X4),
                    lhsT_scale=qq[k][1][:, rows],
                    rhs=hq[k][t][0][:].bitcast(FP8X4),
                    rhs_scale=hq[k][t][1][:],
                    start=first,
                    stop=last,
                )

        def relu(engine, ap):
            if engine == "v":
                nc.vector.tensor_scalar(out=ap, in0=ap, scalar1=0.0, scalar2=None, op0=ALU.max)
            else:
                nc.scalar.activation(out=ap, in_=ap, func=ACT.Relu)

        def finish(t, half, engines):
            rows = stage.tile([P, 2, F], F32, name="out_rows", tag="out_rows", bufs=6, align_bytes=64)
            for i in range(2):
                nc.vector.tensor_tensor(out=rows[:, i, :], in0=z_bank[t, 2 * half + i][:], in1=bias_all[:], op=ALU.add)
            if len(engines) == 2:
                for i in range(2):
                    relu(engines[i], rows[:, i, :])
                    first_row = P * (2 * half + i)
                    nc.sync.dma_start(out=out[t, first_row : first_row + P, :], in_=rows[:, i, :])
            else:
                relu(engines, rows[:])
                nc.sync.dma_start(
                    out=out[t, 2 * P * half : 2 * P * half + 2 * P, :].rearrange("(i p) f -> p i f", p=P), in_=rows[:]
                )

        nc.gpsimd.memset(g_row[:], 0.0)
        nc.gpsimd.memset(e_scales[:].bitcast(I32), 0)
        make_identity(nc, ident_f32[:])
        make_identity(nc, ident_bf16[:])
        nc.gpsimd.memset(ones[:], 1.0)
        load_w(2)
        load_w_factor()
        load_w(1)
        nc.sync.dma_start(out=edge_rows[:], in_=edge.rearrange("(a p) j -> p a j", p=P))
        load_w(0)
        load_x(0)
        load_x(2)
        nc.sync.dma_start(out=g_row[0:1], in_=g.rearrange("(o k) j -> o k j", o=1))
        load_x(1)
        load_x(3)
        load_e()
        nc.sync.dma_start(out=bias_all[:], in_=bias.partition_broadcast(P))
        widen_w(1, "v")
        widen_w(2, "s")
        row_max()
        scale_w(1)
        widen_w(0, "s")
        scale_w(2)
        exponentials(0, 1)
        turn_x(0, "ss")
        turn_x(2, "ss")
        quantize_w(1)
        turn_x(1, "ss")
        turn_x(3, "ss")
        quantize_w(2)
        quantize_x(0)
        column_max_in_partitions()
        quantize_x(1)
        multiply_h(1, 0, 1, "sv")
        scale_w(0)
        column_max()
        logits(0)
        exponentials(0, 0)
        multiply_h(2, 0, 1, "ss")
        multiply_h(1, 0, 0, "sv")
        quantize_x(2)
        quantize_w(0)
        multiply_h(2, 1, 1, "ss")
        exponentials(1, 0)
        logits(1)
        multiply_h(2, 1, 0, "ss")
        multiply_h(0, 0, 1, "sv")
        multiply_h(0, 1, 1, "ss")
        exponentials(2, 1)
        scale_q(0, 0)
        multiply_h(0, 2, 1, "vs")
        multiply_h(2, 2, 1, "sv")
        scale_q(0, 1)
        exponentials(1, 1)
        multiply_h(1, 2, 0, "ss")
        multiply_h(1, 2, 1, "vv")
        scale_q(1, 0)
        turn_q(0, "ss")
        exponentials(2, 0)
        multiply_h(1, 1, 1, "vs")
        multiply_h(0, 0, 0, "vs")
        scale_q(1, 1)
        scale_q(2, 0)
        scale_q(2, 1)
        multiply_h(2, 0, 0, "ss")
        quantize_x(3)
        quantize_h(0, 0)
        multiply_h(0, 1, 0, "ss")
        quantize_q(0)
        multiply_h(0, 2, 0, "ss")
        turn_q(1, "ss")
        quantize_h(1, 0)
        quantize_q(1)
        turn_q(2, "ss")
        multiply_h(1, 1, 0, "ss")
        quantize_h(2, 0)
        multiply_h(0, 3, 1, "vs")
        multiply_z(0, 0, first=True)
        quantize_q(2)
        multiply_z(1, 0)
        multiply_h(2, 2, 0, "ss")
        multiply_z(2, 0, last=True)
        multiply_h(0, 3, 0, "ss")
        quantize_h(0, 1)
        quantize_h(1, 1)
        multiply_h(1, 3, 0, "ss")
        finish(0, 0, "s")
        finish(0, 1, "v")
        multiply_z(1, 1, first=True)
        multiply_z(0, 1)
        quantize_h(2, 1)
        quantize_h(1, 2)
        quantize_h(2, 2)
        multiply_z(2, 1, last=True)
        finish(1, 0, "s")
        multiply_h(1, 3, 1, "ss")
        multiply_h(2, 3, 0, "ss")
        finish(1, 1, "s")
        multiply_z(1, 2, first=True)
        quantize_h(0, 2)
        multiply_z(2, 2)
        multiply_z(0, 2, last=True)
        quantize_h(0, 3)
        multiply_h(2, 3, 1, "ss")
        quantize_h(1, 3)
        finish(2, 0, "s")
        finish(2, 1, "s")
        quantize_h(2, 3)
        multiply_z(0, 3, first=True)
        multiply_z(1, 3)
        multiply_z(2, 3, last=True)
        finish(3, 0, "ss")
        finish(3, 1, "sv")
